import numpy as np, ml_dtypes
CORES = [9,25,41,57]
N = 4
import mx_ref
BF = ml_dtypes.bfloat16
def cut(t, i, w=512):
    return t[:, w * i:w * i + w]
def tile(rs):
    return np.stack(rs, axis=2).reshape(128, -1).astype(BF)
def pick(q, e):
    c = np.concatenate([q[0].reshape(128, -1, 4), np.zeros((128, 1, 4), np.uint8)], axis=1); s = np.concatenate([q[1], np.ones((16, 1), np.uint8)], axis=1)
    return (np.ascontiguousarray(c[:, e].reshape(128, -1)), np.ascontiguousarray(s[:, e]))
def join(*qs):
    return (np.concatenate([q[0] for q in qs], axis=1), np.concatenate([q[1] for q in qs], axis=1))
def put(q, e, v):
    c, s = q[0].reshape(128, -1, 4).copy(), q[1].copy(); c[:, e] = v[0].reshape(128, -1, 4); s[:, e] = v[1]
    return (c.reshape(128, -1), s)
def pk(c, s):
    return (np.ascontiguousarray(c), mx_ref.live(s))
def emit(q):
    return q[0], q[1]
def f(rng, *shape):
    return mx_ref.flush((rng.standard_normal(shape, dtype=np.float32) * np.exp2(rng.integers(-2, 3, shape[:-1] + (1,)))).astype(BF))
def wide(rng, *shape, cols=0):
    v = rng.standard_normal(shape, dtype=np.float32) * np.exp2(rng.integers(-12, 13, shape)).astype(np.float32)
    if cols: v *= np.repeat(np.exp2(rng.integers(-cols, cols + 1, shape[:-2] + (1, shape[-1] // 4))) * (rng.random(shape[:-2] + (1, shape[-1] // 4)) > 0.0625), 4, axis=-1).astype(np.float32)
    return mx_ref.flush(v.astype(BF))
P, S, R = 256, 40, 3
E = P + 2 * S * R
def randoms(rng):
    s = np.where(rng.random((N, P)) < rng.random((N, 1)), -1, 1)
    x = np.abs(f(rng, N, 128, 4 * P).astype(np.float32)) * np.repeat(s, 4, axis=1)[:, None, :].astype(np.float32)
    a = f(rng, N, 128, 512).astype(np.float32) + np.float32(0.05) * rng.standard_normal((N, 1, 1)).astype(np.float32)
    return {"x": mx_ref.flush(x.astype(BF)), "a": mx_ref.flush(a.astype(BF)), "w": f(rng, N, 128, 2048)}
def planted(rng, n, sign):
    up = np.stack([rng.permutation(128) < n[r] for r in range(N)])
    a = (1 + rng.random((N, 128, 512))) * np.exp2(rng.integers(-2, 3, (N, 128, 1))) * np.repeat(np.where(up, 1.0, -1.0), 4, axis=1)[:, None, :]
    x = np.abs(f(rng, N, 128, 4 * P).astype(np.float32)) * np.float32(sign)
    return {"x": x.astype(BF), "a": a.astype(np.float32).astype(BF), "w": f(rng, N, 128, 2048)}
def setup_inputs(rng):
    return randoms(rng)
def setup_inputs_shrink(rng):
    k = N // 2 - int(rng.integers(0, 2))
    n = rng.integers(0, 2, N)
    n[k] = rng.integers(112, 128)
    d = planted(rng, n, 1)
    d["x"][k, :, :4 * S * R] = 0
    d["x"][k, :, 4 * (P - S * R):] = 0
    return d
def setup_inputs_grow(rng):
    k, big = N // 2 - int(rng.integers(0, 2)), int(rng.integers(113, 129))
    less = big if N > 4 else 3 * big // 4
    n = np.full(N, less - 1)
    if k < N // 2: n[:k] = big - 1
    else: n[k + 1:] = big - 1
    n[k] = rng.integers(0, 4)
    return planted(rng, n, 1)
def setup_inputs_spread(rng):
    return {**randoms(rng), "x": wide(rng, N, 128, 4 * P, cols=6)}
def setup_inputs_part(rng):
    k, m = (N - 1) * int(rng.integers(0, 2)), 4 * int(rng.integers(0, 4)) + 2
    d = planted(rng, np.where(np.arange(N) == k, 1, 0), 1)
    on = np.zeros(P, bool)
    on[16 + rng.permutation(P - 32)[:m]] = True
    d["x"][k][:, np.repeat(~on, 4)] = 0
    return d
def setup_inputs_turn(rng):
    k = N // 2 - int(rng.integers(0, 2))
    n = np.full(N, int(rng.integers(112, 128)))
    n[k] = rng.integers(0, 4)
    return planted(rng, n, -1)
def check_inputs(d):
    b = []
    for k in ("x", "a", "w"):
        v = np.abs(d[k].astype(np.float32))
        if not (np.isfinite(v).all() and ((v == 0) | (v >= 2.0 ** -30) & (v <= 2.0 ** 30)).all()): b.append("a value of " + k)
    return b
def held(row, bo, r, m=4):
    e = np.arange(bo[r], bo[r + 1])
    return pick(row, np.concatenate([e, np.full(-e.size % m, -1)]))
def moved(bo, cost):
    before, new = np.concatenate([[0], np.cumsum(cost)]), bo.copy()
    for b in range(1, N):
        g = int(np.argmax(N * before >= b * before[-1]))
        new[b] = bo[b] + min(S, max(-S, g - int(bo[b])))
    return new
def reference(x, a, w):
    qa = [mx_ref.quantize(np.ascontiguousarray(a[r])) for r in range(N)]
    qw = [[mx_ref.quantize(np.ascontiguousarray(cut(w[r], b))) for b in range(4)] for r in range(N)]
    bo, out = P * np.arange(N + 1), []
    row = join(*[mx_ref.quantize(np.ascontiguousarray(x[r])) for r in range(N)])
    for t in range(R):
        cost = []
        for r in range(N):
            z = mx_ref.matmul(qa[r], held(row, bo, r))[:, :bo[r + 1] - bo[r]]
            cost.append(1 + np.sum(z > 0, axis=0).astype(np.int64))
        bo = moved(bo, np.concatenate(cost))
        new = []
        for r in range(N):
            h = held(row, bo, r)
            v = tile([np.maximum(mx_ref.matmul(qw[r][b], h), np.float32(0)) * np.float32(0.0625) for b in range(4)])
            new.append(pick(mx_ref.quantize(np.ascontiguousarray(v)), np.arange(bo[r + 1] - bo[r])))
        row = join(*new)
        out.append(bo)
    y, oc, osc = np.zeros((N, 128, E), np.float32), np.zeros((N, 128, 4 * E), np.uint8), np.zeros((N, 16, E), np.uint8)
    for r in range(N):
        n = int(bo[r + 1] - bo[r])
        y[r, :, :n] = mx_ref.matmul(qa[r], held(row, bo, r))[:, :n]
        oc[r], osc[r] = emit(held(row, bo, r, E))
    return {"y": y, "oc": oc, "osc": osc, "bd": np.stack([np.stack(out).astype(np.float32) for r in range(N)])}

@@ -1,0 +1,410 @@
+import numpy as np
+from concourse.bass import DstId, RemoteDMATransfer
+from concourse.mybir import dt, AluOpType as Op, AxisListType, ActivationFunctionType as Act
+
+F32, BF, I32, U16, F8, U8 = "float32", "bfloat16", "int32", "uint16", "float8_e4m3fn_x4", "uint8"
+SCRATCH = {"ps": ("psum", [128, 4096], F32)}
+for _names, _d in (("xt:1024 at:512 wt:2048 h1:1344 m2:1344 m3:1664 hh1:512 hh2:512 zt:512 junk:1536", BF),
+                   ("eps:4 wts:4 c130:128 nh:32 nha:32 nhb:32 MM:192 XX:96 BBB:96 row:16 rjunk:768 Ball:20 pf:31 j0:31 J:31 J8:8 "
+                    "gi:8 gx:8 cc:12 va:4 vb:8 par:4 kk:16 t8:8 t9:8 terms:192 sum3:96 sum2:32 sum1:32 yt:496 L0:16 L1:16 L2:16 "
+                    "Zq0:128 Zq1:128 Zq2:128 Zh0:128 Zh1:128 Zh2:128 Ih0:128 Ih1:128 Ih2:128", F32),
+                   ("pi:31 pm:31", I32), ("la:8 lb:8 lf:32", U16)):
+    for _s in _names.split():
+        SCRATCH[_s.split(":")[0]] = ("sbuf", [128, int(_s.split(":")[1])], _d)
+for _n, _w in (("qa", 128), ("qw", 512), ("C0", 256), ("C1", 336), ("C2", 464), ("C3", 544), ("H1", 128), ("H2", 128),
+               ("N0", 352), ("N1", 352), ("N2", 352), ("FA", 256), ("FB", 240)):
+    SCRATCH[_n] = ("sbuf", [128, _w], F8)
+    SCRATCH[_n + "s"] = ("sbuf", [128, _w], U8)
+SEMAPHORES = ["sv", "sa", "sp", "gc", "dx0", "dx1", "da", "dw", "dout", "ls"] + \
+    ["%s%d" % (n, t) for n in ("nc", "ns", "lm") for t in range(3)]
+
+
+def rank_program(g, core, T, topo):
+    r = T.rank_of(core)
+    if r is None:
+        return
+    n = len(T.cores)
+    left, right = (r - 1 if r else None), (r + 1 if r < n - 1 else None)
+    base = 256 * r
+    vec, act, ten = g.vector, g.scalar, g.tensor
+    queue = {"v": vec, "a": act, "p": ten, "g": g, "s": g.sync}
+    cnt, seen = {}, {q: {} for q in queue}
+
+    def W(q, *toks):
+        need = {}
+        for s, c in toks:
+            need[s] = max(need.get(s, 0), c)
+        for s, c in need.items():
+            if seen[q].get(s, 0) < c:
+                queue[q].wait_ge(T.sem[s], c)
+                seen[q][s] = c
+
+    def inc(sem, ins, k=1):
+        ins.then_inc(T.sem[sem], k)
+        cnt[sem] = cnt.get(sem, 0) + k
+        return (sem, cnt[sem])
+
+    V = lambda ins: inc("sv", ins)
+    A = lambda ins: inc("sa", ins)
+    P = lambda ins: inc("sp", ins)
+    G = lambda ins: inc("gc", ins)
+    bank = lambda k, a, b: T.ps[:, 512 * k + a:512 * k + b]
+
+    def nbs(q):
+        return [p for p in (q - 1, q + 1) if 0 <= p < n]
+
+    def engs(q, p):
+        e = topo.engines(T.cores[q], T.cores[p])
+        k = len(e) // len(nbs(q))
+        i = nbs(q).index(p)
+        return e[k * i:k * i + k]
+
+    def did(p):
+        rid, pnc, _ = topo.addr(T.cores[p])
+        return DstId(rid=rid, pnc=pnc)
+
+    def send_ends(t, src, name, lo, hi):
+        tr = []
+        for p in nbs(r):
+            a, c = (lo, 176) if p < r else (hi, 128)
+            if name == "nc":
+                s, d = src[:, a:a + 48].bitcast(dt.uint8), T["N%d" % t][:, c:c + 48].bitcast(dt.uint8)
+            else:
+                s, d = src[:, a:a + 48], T["N%ds" % t][:, c:c + 48]
+            e = engs(r, p)
+            tr.append(RemoteDMATransfer(dst_ids=[did(p)], dma_engine_mask=sum(1 << i for i in e),
+                                        remote_sem=T.sem["%s%d" % (name, t)], src=s, dst=d))
+            cnt["ls"] = cnt.get("ls", 0) + len(e)
+        g.remote_dma_fused(tr, local_sem=T.sem.ls)
+
+    others = [p for p in range(n) if p != r]
+
+    def send_costs(t):
+        s = T["L%d" % t][:, 4 * r:4 * r + 4]
+        e = topo.engines(T.cores[r], T.cores[others[0]])
+        g.remote_dma_fused([RemoteDMATransfer(dst_ids=[did(p) for p in others], dma_engine_mask=sum(1 << i for i in e),
+                                              remote_sem=T.sem["lm%d" % t], srcs=[s], dsts=[s for p in others])],
+                           local_sem=T.sem.ls)
+        cnt["ls"] = cnt.get("ls", 0) + len(e)
+
+    n_in = sum(len(engs(p, r)) for p in nbs(r))
+    l_in = sum(len(topo.engines(T.cores[p], T.cores[r])) for p in others)
+
+    kx0 = inc("dx0", g.sync.dma_start(T.xt[:, 0:512], T.x[:, 0:512]), 16)
+    kx1 = inc("dx1", act.dma_start(T.xt[:, 512:1024], T.x[:, 512:1024]), 16)
+    ka = inc("da", g.sync.dma_start(T.at[:], T.a[:]), 16)
+    inc("dw", act.dma_start(T.wt[:, 1024:2048], T.w[:, 1024:2048]), 16)
+    kw = inc("dw", g.sync.dma_start(T.wt[:, 0:1024], T.w[:, 0:1024]), 16)
+
+    veps = V(vec.memset(T.eps[:, 0:1], -(2.0 ** -120)))
+    V(vec.memset(T.row[0:5, 0:1], -0.125))
+    for b in range(1, n):
+        V(vec.memset(T.wts[:, b - 1:b], b / 4.0 - (1.0 if r < b else 0.0)))
+    vnh = V(vec.memset(T.nh[0:32, :], -0.5))
+    V(vec.memset(T.c130[0:32, :], 130.0))
+    V(vec.memset(T.XX[0:32, :], 0.0))
+    vset = V(vec.memset(T.MM[:], 0.0))
+    G(g.iota(T.Ball[:, 0:5], [[256, 5]], 0, 0, allow_small_or_imprecise_dtypes=True))
+    G(g.iota(T.pi[:], [[0, 31]], 0, 1))
+    G(g.iota(T.j0[:], [[16, 31]], 0, 0, allow_small_or_imprecise_dtypes=True))
+    for k, (b0, cm) in enumerate(((base - 40, 1), (base + 88, 1), (base + 168, 1), (40, -1), (40, -1))):
+        gk = G(g.iota(T.gi[:, k:k + 1], [[0, 1]], b0, cm, allow_small_or_imprecise_dtypes=True))
+    W("g", gk, vnh)
+    G(g.affine_select(T.gx[:, 2:3], T.gi[:, 2:3], [[0, 1]], Op.is_ge, 1e6, -48, 1))
+    G(g.affine_select(T.gx[:, 3:4], T.gi[:, 3:4], [[0, 1]], Op.is_ge, 1e6, 39, -1))
+    G(g.affine_select(T.gx[:, 5:6], T.gi[:, 4:5], [[0, 1]], Op.is_ge, -1e6, 79, -1))
+    gk = G(g.affine_select(T.nha[0:32, :], T.nh[0:32, :], [[0, 32]], Op.is_ge, 0.0, -1, 1))
+    W("g", gk)
+    G(g.affine_select(T.gx[:, 4:5], T.gx[:, 5:6], [[0, 1]], Op.is_ge, -1e6, -40, 1))
+    gset = G(g.affine_select(T.nhb[0:32, :], T.nha[0:32, :], [[0, 32]], Op.is_ge, 0.0, n - 1, -1))
+
+    W("v", kx0)
+    V(vec.quantize_mx(T.C0[:, 0:128], T.C0s[:, 0:128], T.xt[:, 0:512]))
+    W("v", kx1)
+    vx = V(vec.quantize_mx(T.C0[:, 128:256], T.C0s[:, 128:256], T.xt[:, 512:1024]))
+    W("v", ka)
+    va = V(vec.quantize_mx(T.qa[:], T.qas[:], T.at[:]))
+    W("g", vx)
+    send_ends(0, T.C0, "nc", 0, 208)
+
+    def cost_mm(k, C, Cs, a):
+        return P(ten.matmul_mx(bank(k, 0, 128), C[:, a:a + 128], Cs[:, a:a + 128], T.qa[:], T.qas[:], True, True))
+
+    junk = []
+
+    def count(out, k):
+        j = 128 * len(junk)
+        junk.append(j)
+        return A(act.activation(T.junk[:, j:j + 128], bank(k, 0, 128), Act.Sign, bias=T.eps[:, 0:1], accum_out=out))
+
+    W("p", va)
+    p0, p1 = cost_mm(4, T.C0, T.C0s, 0), cost_mm(5, T.C0, T.C0s, 128)
+    W("a", p0, veps)
+    a0 = count(T.cc[:, 0:1], 4)
+    W("a", p1)
+    a1 = count(T.cc[:, 1:2], 5)
+    W("v", a1)
+    vp = V(vec.tensor_tensor(T.par[:, 0:1], T.cc[:, 0:1], T.cc[:, 1:2], Op.add))
+    V(vec.tensor_copy(T.L0[0:64, 4 * r + 3:4 * r + 4], T.cc[0:64, 0:1]))
+    V(vec.tensor_copy(T.L0[64:128, 4 * r + 3:4 * r + 4], T.cc[64:128, 1:2]))
+    W("v", vp)
+    vq = V(vec.tensor_scalar(T.L0[:, 4 * r:4 * r + 3], T.wts[:, 0:3], T.par[:, 0:1], None, Op.mult))
+    own = [vq]
+    W("g", vq)
+    send_costs(0)
+    send_ends(0, T.C0s, "ns", 0, 208)
+
+    W("v", kw)
+    vw = V(vec.quantize_mx(T.qw[:], T.qws[:], T.wt[:]))
+
+    def w_mm(k, b, C, Cs, a, m):
+        return P(ten.matmul_mx(bank(k, 0, m), T.qw[:, 128 * b:128 * b + 128], T.qws[:, 128 * b:128 * b + 128],
+                               C[:, a:a + m], Cs[:, a:a + m], True, True))
+
+    def own_mm(C, Cs, m, frees):
+        W("p", *frees)
+        return [w_mm(b, b, C, Cs, 0, m) for b in range(4)]
+
+    def relu(q, out, src):
+        if q == "a":
+            return A(act.activation(out, src, Act.Relu, scale=0.0625))
+        return V(vec.tensor_scalar(out, src, 0.0, 0.0625, Op.max, Op.mult))
+
+    def own_relu(pm, h, at, m):
+        out = []
+        for b, q in ((0, "a"), (1, "v"), (2, "a"), (3, "v")):
+            W(q, pm[b])
+            out.append(relu(q, h[:, 4 * at + b:4 * (at + m):4], bank(b, 0, m)))
+        return out
+
+    pm = own_mm(T.C0, T.C0s, 256, [vx, vw])
+    W("v", V(vec.memset(T.zt[:], 0.0)))
+
+    def zero_pads(t):
+        for a in ([48] if left is None else []) + [224 if right is not None else 176]:
+            out = V(vec.quantize_mx(T["N%d" % t][:, a:a + 128], T["N%ds" % t][:, a:a + 128], T.zt[:]))
+        return out
+    vpad = [zero_pads(0)]
+    rl = own_relu(pm, T.h1, 40, 256)
+    W("v", gset)
+    W("v", V(vec.tensor_scalar(T.pm[:], T.pi[:], 15, None, Op.bitwise_and)))
+    W("v", V(vec.tensor_copy(T.pf[:], T.pm[:])))
+    W("v", V(vec.tensor_tensor(T.J[:], T.j0[:], T.pf[:], Op.add)))
+    V(vec.tensor_copy(T.J8[:, 0:4], T.J[:, 0:4]))
+    V(vec.tensor_scalar(T.J8[:, 4:8], T.J[:, 0:4], -64.0, None, Op.add))
+    vpad += [zero_pads(1), zero_pads(2)]
+    V(vec.memset(T.hh1[:, 320:512], 0.0))
+    vh = V(vec.memset(T.hh2[:, 320:512], 0.0))
+
+    def halo_mm(t, frees):
+        W("p", vpad[t], *frees)
+        W("p", ("nc%d" % t, n_in), ("ns%d" % t, n_in))
+        return [w_mm(4 + b, b, T["N%d" % t], T["N%ds" % t], 128, 128) for b in range(4)]
+
+    def borders(t, own, act_mid, vec_mid):
+        Lt, Zq, Zh, Ih = T["L%d" % t], T["Zq%d" % t], T["Zh%d" % t], T["Ih%d" % t]
+        mo = 64 * t
+        rj = 256 * t
+        lm = ("lm%d" % t, l_in)
+        W("a", lm, vset, *own)
+        A(act.activation(T.MM[64:128, mo + 33:mo + 36], Lt[64:128, 3:12:4], Act.Copy))
+        ac = A(act.activation(T.MM[0:64, mo + 33:mo + 36], Lt[0:64, 7:16:4], Act.Copy))
+        W("v", lm, vset, *own)
+        for b in range(1, n):
+            vr = V(vec.tensor_reduce(T.MM[:, mo + b:mo + b + 1], Lt[:, b - 1:16:4], AxisListType.X, Op.add))
+        mids = act_mid()
+        W("v", vr)
+        for k in range(4):
+            vt = V(vec.transpose(Zq[0:32, 32 * k:32 * k + 32], T.MM[32 * k:32 * k + 32, mo:mo + 32]))
+        W("a", vt)
+        aq = A(act.activation(T.rjunk[0:5, rj:rj + 128], Zq[0:5, :], Act.Copy, accum_out=T.row[0:5, 4 + t:5 + t]))
+        W("v", ac)
+        for k in range(4):
+            z = (k + 2) % 4
+            vt = V(vec.transpose(Zh[0:32, 32 * z:32 * z + 32], T.MM[32 * k:32 * k + 32, mo + 32:mo + 64]))
+        W("v", vt)
+        vs = V(vec.tensor_tensor_scan(Ih[0:5, :], Zh[0:5, :], T.c130[0:5, :], 0.0, Op.add, Op.add))
+        W("v", vs, aq)
+        vb = V(vec.tensor_scalar(T.row[0:5, 7 + t:8 + t], Ih[0:5, 63:64], T.row[0:5, 4 + t:5 + t], T.row[0:5, t:t + 1],
+                                 Op.add, Op.add))
+        W("a", vb)
+        av = A(act.activation(T.rjunk[0:5, rj + 128:rj + 208], Ih[0:5, 23:103], Act.Sign, bias=T.row[0:5, 7 + t:8 + t],
+                              scale=-1.0, accum_out=T.row[0:5, 10 + t:11 + t]))
+        vm = vec_mid(mids)
+        W("v", av, gset)
+        W("v", V(vec.tensor_scalar(T.XX[0:5, 32 * t:32 * t + 32], T.nhb[0:5, :], T.row[0:5, 10 + t:11 + t], None, Op.mult)))
+        for k in range(4):
+            vB = V(vec.transpose(T.BBB[32 * k:32 * k + 32, 32 * t:32 * t + 32], T.XX[0:32, 32 * t:32 * t + 32]))
+        if t < 2:
+            V(vec.tensor_scalar(T.row[0:5, t + 1:t + 2], T.row[0:5, 10 + t:11 + t], -65.0, T.row[0:5, t:t + 1],
+                                Op.mult, Op.add))
+        W("v", vB)
+        vN = V(vec.tensor_tensor(T.Ball[:, 5 * t + 5:5 * t + 10], T.Ball[:, 5 * t:5 * t + 5],
+                                 T.BBB[:, 32 * t:32 * t + 5], Op.subtract))
+        return vm, vB, vN
+
+    Bl = lambda t: T.Ball[:, 5 * t + r:5 * t + r + 1]
+    Br = lambda t: T.Ball[:, 5 * t + r + 1:5 * t + r + 2]
+    el = lambda t: T.BBB[:, 32 * t + r:32 * t + r + 1]
+    er = lambda t: T.BBB[:, 32 * t + r + 1:32 * t + r + 2]
+
+    def pick_ends(t, C, Cs, m, lst, vl, frees):
+        H, Hs = T["H%d" % t], T["H%ds" % t]
+        W("v", vl, *frees)
+        vp = V(vec.tensor_copy(H[:, 0:128].bitcast(dt.uint32), C[:, 0:m].bitcast(dt.uint32).indirect(lst[:, 0:8])))
+        W("a", vl, *frees)
+        ap = A(act.activation(Hs[:, 0:128], Cs[:, 0:m].indirect(lst[:, 0:8]), Act.Copy))
+        W("g", vp)
+        send_ends(t, H, "nc", 0, 80)
+        W("p", vp, ap)
+        ph = cost_mm(4, H, Hs, 0)
+        W("a", ph)
+        return ap, count(T["L%d" % t][:, 4 * r + 3:4 * r + 4], 4)
+
+    def finish_costs(t, vtile, k, toks, ap, ac):
+        W("v", *toks)
+        W("v", V(vec.tensor_reduce(T.par[:, t:t + 1], vtile[:, 0:k], AxisListType.X, Op.add)))
+        vq = V(vec.tensor_scalar(T["L%d" % t][:, 4 * r:4 * r + 3], T.wts[:, 0:3], T.par[:, t:t + 1], None, Op.mult))
+        W("g", vq, ac)
+        send_costs(t)
+        W("g", ap)
+        send_ends(t, T["H%ds" % t], "ns", 0, 80)
+        return [vq, ac]
+
+    ph0 = halo_mm(0, [a0, a1])
+
+    def mid0():
+        out = []
+        for b in range(4):
+            W("a", ph0[b])
+            out.append(relu("a", T.h1[:, b:160:4], bank(4 + b, 8, 48)))
+            out.append(relu("a", T.h1[:, 1184 + b:1344:4], bank(4 + b, 48, 88)))
+        return out
+
+    def q1(mids):
+        W("v", *mids, *rl)
+        return V(vec.quantize_mx(T.C1[:], T.C1s[:], T.h1[:]))
+    vm, vB, vN = borders(0, own, mid0, q1)
+    W("p", vm)
+    pc = [cost_mm(k, T.C1, T.C1s, a) for k, a in enumerate((0, 128, 208))]
+    ac = []
+    for k, out in enumerate((T.cc[:, 2:3], T.va[:, 1:2], T.cc[:, 3:4])):
+        W("a", pc[k])
+        ac.append(count(out, k))
+    V(vec.tensor_scalar(T.la[:, 0:4], T.J8[:, 0:4], el(0), 40.0, Op.subtract, Op.add))
+    vl = V(vec.tensor_scalar(T.la[:, 4:8], T.J8[:, 4:8], er(0), 296.0, Op.subtract, Op.add))
+    ap, ach = pick_ends(1, T.C1, T.C1s, 336, T.la, vl, [vm])
+    W("v", vN, *ac)
+    V(vec.tensor_scalar(T.va[:, 0:1], T.gi[:, 0:1], Bl(1), T.cc[:, 2:3], Op.is_ge, Op.mult))
+    vv = V(vec.tensor_scalar(T.va[:, 2:3], T.gx[:, 2:3], Br(1), T.cc[:, 3:4], Op.is_lt, Op.mult))
+    own = finish_costs(1, T.va, 3, [vv], ap, ach)
+
+    pm = own_mm(T.C1, T.C1s, 336, [vm, *ac])
+    rl = own_relu(pm, T.m2, 0, 336)
+    W("v", *rl)
+    vc2 = V(vec.quantize_mx(T.C2[:, 0:336], T.C2s[:, 0:336], T.m2[:]))
+    vk1 = V(vec.tensor_scalar(T.kk[:, 0:2], T.Ball[:, 5 + r:7 + r], -1.0, float(336 + base), Op.mult, Op.add))
+    W("p", vc2)
+    pc = [cost_mm(k, T.C2, T.C2s, a) for k, a in enumerate((0, 128, 208))]
+    ac = []
+    for k in range(3):
+        W("a", pc[k])
+        ac.append(count(T.cc[:, 4 + k:5 + k], k))
+    ph1 = halo_mm(1, [ach])
+
+    def halo_relus(ph, hh):
+        def f():
+            out = []
+            for b in range(4):
+                W("a", ph[b])
+                out.append(relu("a", hh[:, b:320:4], bank(4 + b, 8, 88)))
+            return out
+        return f
+
+    def q2(mids):
+        W("v", vh, *mids)
+        return V(vec.quantize_mx(T.C2[:, 336:464], T.C2s[:, 336:464], T.hh1[:]))
+    vm, vB, vN = borders(1, own, halo_relus(ph1, T.hh1), q2)
+    W("p", vm)
+    ppc = cost_mm(3, T.C2, T.C2s, 336)
+    W("a", ppc)
+    ac.append(count(T.cc[:, 7:8], 3))
+    W("v", vB, vk1)
+    V(vec.tensor_scalar(T.t8[:, 0:4], T.J8[:, 0:4], el(1), T.kk[:, 0:1], Op.is_lt, Op.mult))
+    W("v", V(vec.tensor_scalar(T.t8[:, 4:8], T.J8[:, 4:8], er(1), T.kk[:, 1:2], Op.is_ge, Op.mult)))
+    W("v", V(vec.tensor_tensor(T.t9[:], T.t8[:], T.J8[:], Op.add)), vN)
+    V(vec.tensor_scalar(T.lb[:, 0:4], T.t9[:, 0:4], Bl(2), float(40 - base), Op.add, Op.add))
+    vl = V(vec.tensor_scalar(T.lb[:, 4:8], T.t9[:, 4:8], Br(2), float(40 - base), Op.add, Op.add))
+    ap, ach = pick_ends(2, T.C2, T.C2s, 416, T.lb, vl, [vm, vc2])
+    V(vec.tensor_tensor(T.kk[:, 4:5], Bl(1), Bl(2), Op.max))
+    v1 = V(vec.tensor_tensor(T.kk[:, 5:6], Br(1), Br(2), Op.min))
+    W("v", *ac)
+    V(vec.tensor_scalar(T.vb[:, 3:4], T.gx[:, 3:4], el(1), T.cc[:, 7:8], Op.is_le, Op.mult))
+    V(vec.tensor_scalar(T.vb[:, 4:5], T.gx[:, 4:5], er(1), T.cc[:, 7:8], Op.is_gt, Op.mult))
+    W("v", v1)
+    V(vec.tensor_scalar(T.vb[:, 0:1], T.gi[:, 0:1], T.kk[:, 4:5], T.cc[:, 4:5], Op.is_ge, Op.mult))
+    V(vec.tensor_scalar(T.vb[:, 1:2], T.gi[:, 1:2], T.kk[:, 5:6], T.cc[:, 5:6], Op.is_lt, Op.mult))
+    vv = V(vec.tensor_scalar(T.vb[:, 2:3], T.gx[:, 2:3], T.kk[:, 5:6], T.cc[:, 6:7], Op.is_lt, Op.mult))
+    own = finish_costs(2, T.vb, 5, [vv], ap, ach)
+
+    pm = own_mm(T.C2, T.C2s, 416, [vm, vc2, *ac])
+    W("v", V(vec.tensor_scalar(T.kk[:, 2:4], T.Ball[:, 10 + r:12 + r], -1.0, float(416 + base), Op.mult, Op.add)))
+    vk3 = V(vec.tensor_tensor(T.kk[:, 6:8], T.kk[:, 2:4], T.kk[:, 0:2], Op.subtract))
+    rl = own_relu(pm, T.m3, 0, 416)
+    W("v", *rl)
+    vc3 = V(vec.quantize_mx(T.C3[:, 0:416], T.C3s[:, 0:416], T.m3[:]))
+    ph2 = halo_mm(2, [ach])
+
+    def q3(mids):
+        W("v", vh, *mids)
+        return V(vec.quantize_mx(T.C3[:, 416:544], T.C3s[:, 416:544], T.hh2[:]))
+    vm, vB, vN = borders(2, own, halo_relus(ph2, T.hh2), q3)
+    W("v", vN)
+    U = T.terms[:, 0:31]
+    W("v", V(vec.tensor_scalar(U, T.J[:], Bl(3), None, Op.add)), vk3)
+    V(vec.tensor_scalar(T.terms[:, 31:62], U, Bl(2), T.kk[:, 6:7], Op.is_lt, Op.mult))
+    V(vec.tensor_scalar(T.terms[:, 62:93], U, T.kk[:, 4:5], T.kk[:, 0:1], Op.is_lt, Op.mult))
+    V(vec.tensor_scalar(T.terms[:, 93:124], U, Br(2), T.kk[:, 7:8], Op.is_ge, Op.mult))
+    V(vec.tensor_scalar(T.terms[:, 124:155], U, T.kk[:, 5:6], T.kk[:, 1:2], Op.is_ge, Op.mult))
+    W("v", V(vec.tensor_scalar(T.terms[:, 155:186], U, Br(3), 2000.0, Op.is_ge, Op.mult)))
+    W("v", V(vec.tensor_tensor(T.sum3[:, 0:93], T.terms[:, 0:93], T.terms[:, 93:186], Op.add)))
+    W("v", V(vec.tensor_tensor(T.sum2[:, 0:31], T.sum3[:, 0:31], T.sum3[:, 31:62], Op.add)))
+    W("v", V(vec.tensor_tensor(T.sum1[:, 0:31], T.sum2[:, 0:31], T.sum3[:, 62:93], Op.add)))
+    vl = V(vec.tensor_scalar(T.lf[:, 0:31], T.sum1[:, 0:31], float(40 - base), 500.0, Op.add, Op.min))
+    W("s", vN)
+    inc("dout", g.sync.dma_start(T.bd[:], T.Ball[0:1, 5:20]), 16)
+    W("v", vl, vm, vc3)
+    W("a", vl, vm, vc3)
+    halves = (("FA", 0, 256), ("FB", 256, 496))
+    vf, af, py = [], [], []
+    for F, a, b in halves:
+        l = T.lf[:, a // 16:b // 16]
+        vf.append(V(vec.tensor_copy(T[F][:].bitcast(dt.uint32), T.C3[:, 0:544].bitcast(dt.uint32).indirect(l))))
+        af.append(A(act.activation(T[F + "s"][:], T.C3s[:, 0:544].indirect(l), Act.Copy)))
+    for k, (F, a, b) in enumerate(halves):
+        W("p", vf[k], af[k])
+        py.append(P(ten.matmul_mx(bank(k, 0, b - a), T.qa[:], T.qas[:], T[F][:], T[F + "s"][:], True, True)))
+    W("v", py[0])
+    vy = V(vec.tensor_copy(T.yt[:, 0:256], bank(0, 0, 256)))
+    W("a", py[1])
+    ay = A(act.activation(T.yt[:, 256:496], bank(1, 0, 240), Act.Copy))
+
+    def out_codes(k):
+        F, a, b = halves[k]
+        W("s", vf[k])
+        inc("dout", g.sync.dma_start(T.oc[:, 4 * a:4 * b], T[F][:].bitcast(dt.uint8)), 16)
+
+    def out_scales(q, k):
+        F, a, b = halves[k]
+        W(q, af[k])
+        for i in range(4):
+            inc("dout", queue[q].dma_start(T.osc[4 * i:4 * i + 4, a:b], T[F + "s"][32 * i:32 * i + 4, :]), 16)
+    out_codes(0)
+    out_scales("s", 0)
+    out_codes(1)
+    W("s", vy)
+    inc("dout", g.sync.dma_start(T.y[:, 0:256], T.yt[:, 0:256]), 16)
+    W("a", ay)
+    inc("dout", act.dma_start(T.y[:, 256:496], T.yt[:, 256:496]), 16)
+    out_scales("a", 1)
+    W("g", *[(s, c) for s, c in cnt.items()])

@@ -4,19 +4,22 @@ from concourse.mybir import dt, AluOpType as Op, AxisListType, ActivationFunctio
 
 F32, BF, I32, U16, F8, U8 = "float32", "bfloat16", "int32", "uint16", "float8_e4m3fn_x4", "uint8"
 SCRATCH = {"ps": ("psum", [128, 4096], F32)}
-for _names, _d in (("xt:1024 at:512 wt:2048 h1:1344 m2:1344 m3:1664 hh1:512 hh2:512 zt:512 junk:1536", BF),
-                   ("eps:4 wts:4 c130:128 nh:32 nha:32 nhb:32 MM:192 XX:96 BBB:96 row:16 rjunk:768 Ball:20 pf:31 j0:31 J:31 J8:8 "
-                    "gi:8 gx:8 cc:12 va:4 vb:8 par:4 kk:16 t8:8 t9:8 terms:192 sum3:96 sum2:32 sum1:32 yt:496 L0:16 L1:16 L2:16 "
-                    "Zq0:128 Zq1:128 Zq2:128 Zh0:128 Zh1:128 Zh2:128 Ih0:128 Ih1:128 Ih2:128", F32),
-                   ("pi:31 pm:31", I32), ("la:8 lb:8 lf:32", U16)):
+for _names, _d in (("xt:1024 at:512 wt:2048 h1:1536 m2:2048 m3:1664 hh2:512 zt:512 junk:1280", BF),
+                   ("eps:4 kb:4 c130:256 nh:32 nha:32 nhb:32 MM:288 XX:96 lo:96 hi:4 BBB:96 row:16 rjunk:1536 B0:5 Bh:16 Ball:16 "
+                    "pf:31 j0:31 J:31 J2:31 J2m:31 JL:8 JR:8 Jm:16 J8:8 gi:4 WT0:48 WT1:48 MK1:16 MK2:16 MW1:48 MW2:48 "
+                    "LW:144 LM:48 t1:16 t2:16 kk:4 terms:192 sum3:64 sum1:32 yt:496 L0:16 L1:16 L2:16 "
+                    "Zq0:128 Zq1:128 Zq2:128 Zh0:128 Zh1:160 Zh2:256 Ih0:132 Ih1:164 Ih2:244", F32),
+                   ("pi:31 pm:31", I32), ("la:16 lb:8 lf:32", U16)):
     for _s in _names.split():
         SCRATCH[_s.split(":")[0]] = ("sbuf", [128, int(_s.split(":")[1])], _d)
-for _n, _w in (("qa", 128), ("qw", 512), ("C0", 256), ("C1", 336), ("C2", 464), ("C3", 544), ("H1", 128), ("H2", 128),
-               ("N0", 352), ("N1", 352), ("N2", 352), ("FA", 256), ("FB", 240)):
+for _n, _w in (("qa", 128), ("qw", 512), ("C0", 256), ("W1", 640), ("M1", 256), ("C2", 512), ("C3", 544), ("H2", 128),
+               ("N0", 352), ("N2", 352), ("FA", 256), ("FB", 240)):
     SCRATCH[_n] = ("sbuf", [128, _w], F8)
     SCRATCH[_n + "s"] = ("sbuf", [128, _w], U8)
 SEMAPHORES = ["sv", "sa", "sp", "gc", "dx0", "dx1", "da", "dw", "dout", "ls"] + \
     ["%s%d" % (n, t) for n in ("nc", "ns", "lm") for t in range(3)]
+HALF = (64, 80, 120)
+MOVE = (40, 80, 120)
 
 
 def rank_program(g, core, T, topo):
@@ -25,7 +28,6 @@ def rank_program(g, core, T, topo):
         return
     n = len(T.cores)
     left, right = (r - 1 if r else None), (r + 1 if r < n - 1 else None)
-    base = 256 * r
     vec, act, ten = g.vector, g.scalar, g.tensor
     queue = {"v": vec, "a": act, "p": ten, "g": g, "s": g.sync}
     cnt, seen = {}, {q: {} for q in queue}
@@ -63,14 +65,14 @@ def rank_program(g, core, T, topo):
         rid, pnc, _ = topo.addr(T.cores[p])
         return DstId(rid=rid, pnc=pnc)
 
-    def send_ends(t, src, name, lo, hi):
+    def send_ends(t, name, src, dst, w, to_left, to_right):
         tr = []
         for p in nbs(r):
-            a, c = (lo, 176) if p < r else (hi, 128)
+            a, c = to_left if p < r else to_right
             if name == "nc":
-                s, d = src[:, a:a + 48].bitcast(dt.uint8), T["N%d" % t][:, c:c + 48].bitcast(dt.uint8)
+                s, d = T[src][:, a:a + w].bitcast(dt.uint8), T[dst][:, c:c + w].bitcast(dt.uint8)
             else:
-                s, d = src[:, a:a + 48], T["N%ds" % t][:, c:c + 48]
+                s, d = T[src + "s"][:, a:a + w], T[dst + "s"][:, c:c + w]
             e = engs(r, p)
             tr.append(RemoteDMATransfer(dst_ids=[did(p)], dma_engine_mask=sum(1 << i for i in e),
                                         remote_sem=T.sem["%s%d" % (name, t)], src=s, dst=d))
@@ -96,26 +98,23 @@ def rank_program(g, core, T, topo):
     inc("dw", act.dma_start(T.wt[:, 1024:2048], T.w[:, 1024:2048]), 16)
     kw = inc("dw", g.sync.dma_start(T.wt[:, 0:1024], T.w[:, 0:1024]), 16)
 
+    vnh = V(vec.memset(T.nh[0:32, :], 80.0))
+    for t in range(3):
+        V(vec.memset(T["L%d" % t][:, 4 * r:4 * r + 4], 0.0))
     veps = V(vec.memset(T.eps[:, 0:1], -(2.0 ** -120)))
-    V(vec.memset(T.row[0:5, 0:1], -0.125))
     for b in range(1, n):
-        V(vec.memset(T.wts[:, b - 1:b], b / 4.0 - (1.0 if r < b else 0.0)))
-    vnh = V(vec.memset(T.nh[0:32, :], -0.5))
-    V(vec.memset(T.c130[0:32, :], 130.0))
-    V(vec.memset(T.XX[0:32, :], 0.0))
-    vset = V(vec.memset(T.MM[:], 0.0))
-    G(g.iota(T.Ball[:, 0:5], [[256, 5]], 0, 0, allow_small_or_imprecise_dtypes=True))
+        k, c = 16 * (b - 1), 4 * (b - 1) + 2
+        V(vec.memset(T.WT1[:, k:k + c], 1 - b / 4.0))
+        V(vec.memset(T.WT1[:, k + c:k + 16], -b / 4.0))
+    V(vec.memset(T.MK1[:], 1.0))
     G(g.iota(T.pi[:], [[0, 31]], 0, 1))
     G(g.iota(T.j0[:], [[16, 31]], 0, 0, allow_small_or_imprecise_dtypes=True))
-    for k, (b0, cm) in enumerate(((base - 40, 1), (base + 88, 1), (base + 168, 1), (40, -1), (40, -1))):
-        gk = G(g.iota(T.gi[:, k:k + 1], [[0, 1]], b0, cm, allow_small_or_imprecise_dtypes=True))
-    W("g", gk, vnh)
-    G(g.affine_select(T.gx[:, 2:3], T.gi[:, 2:3], [[0, 1]], Op.is_ge, 1e6, -48, 1))
-    G(g.affine_select(T.gx[:, 3:4], T.gi[:, 3:4], [[0, 1]], Op.is_ge, 1e6, 39, -1))
-    G(g.affine_select(T.gx[:, 5:6], T.gi[:, 4:5], [[0, 1]], Op.is_ge, -1e6, 79, -1))
+    G(g.iota(T.B0[:], [[256, 5]], 0, 0, allow_small_or_imprecise_dtypes=True))
+    for k, b0 in enumerate((-160, -240, 16)):
+        G(g.iota(T.gi[:, k:k + 1], [[0, 1]], b0, 2, allow_small_or_imprecise_dtypes=True))
+    W("g", vnh)
     gk = G(g.affine_select(T.nha[0:32, :], T.nh[0:32, :], [[0, 32]], Op.is_ge, 0.0, -1, 1))
     W("g", gk)
-    G(g.affine_select(T.gx[:, 4:5], T.gx[:, 5:6], [[0, 1]], Op.is_ge, -1e6, -40, 1))
     gset = G(g.affine_select(T.nhb[0:32, :], T.nha[0:32, :], [[0, 32]], Op.is_ge, 0.0, n - 1, -1))
 
     W("v", kx0)
@@ -125,265 +124,334 @@ def rank_program(g, core, T, topo):
     W("v", ka)
     va = V(vec.quantize_mx(T.qa[:], T.qas[:], T.at[:]))
     W("g", vx)
-    send_ends(0, T.C0, "nc", 0, 208)
+    send_ends(0, "nc", "C0", "N0", 48, (0, 176), (208, 128))
 
-    def cost_mm(k, C, Cs, a):
-        return P(ten.matmul_mx(bank(k, 0, 128), C[:, a:a + 128], Cs[:, a:a + 128], T.qa[:], T.qas[:], True, True))
+    def cost_mm(k, name, a):
+        return P(ten.matmul_mx(bank(k, 0, 128), T[name][:, a:a + 128], T[name + "s"][:, a:a + 128], T.qa[:], T.qas[:], True, True))
 
     junk = []
 
-    def count(out, k):
+    def count(t, piece, k, tok):
+        W("a", tok)
         j = 128 * len(junk)
         junk.append(j)
-        return A(act.activation(T.junk[:, j:j + 128], bank(k, 0, 128), Act.Sign, bias=T.eps[:, 0:1], accum_out=out))
+        c = 4 * r + piece
+        return A(act.activation(T.junk[:, j:j + 128], bank(k, 0, 128), Act.Sign, bias=T.eps[:, 0:1],
+                                accum_out=T["L%d" % t][:, c:c + 1]))
 
     W("p", va)
-    p0, p1 = cost_mm(4, T.C0, T.C0s, 0), cost_mm(5, T.C0, T.C0s, 128)
-    W("a", p0, veps)
-    a0 = count(T.cc[:, 0:1], 4)
-    W("a", p1)
-    a1 = count(T.cc[:, 1:2], 5)
-    W("v", a1)
-    vp = V(vec.tensor_tensor(T.par[:, 0:1], T.cc[:, 0:1], T.cc[:, 1:2], Op.add))
-    V(vec.tensor_copy(T.L0[0:64, 4 * r + 3:4 * r + 4], T.cc[0:64, 0:1]))
-    V(vec.tensor_copy(T.L0[64:128, 4 * r + 3:4 * r + 4], T.cc[64:128, 1:2]))
-    W("v", vp)
-    vq = V(vec.tensor_scalar(T.L0[:, 4 * r:4 * r + 3], T.wts[:, 0:3], T.par[:, 0:1], None, Op.mult))
-    own = [vq]
-    W("g", vq)
+    p0, p1 = cost_mm(4, "C0", 0), cost_mm(5, "C0", 128)
+    W("a", veps)
+    a0 = count(0, 0, 4, p0)
+    a1 = count(0, 1, 5, p1)
+    W("g", a1)
     send_costs(0)
-    send_ends(0, T.C0s, "ns", 0, 208)
+    send_ends(0, "ns", "C0", "N0", 48, (0, 176), (208, 128))
 
+    vmm = V(vec.memset(T.MM[:], 0.0))
+    V(vec.memset(T.zt[:], 0.0))
+    for b in range(1, n):
+        k, c = 16 * (b - 1), 4 * (b - 1) + 2
+        V(vec.memset(T.WT0[:, k:k + c], 1 - b / 4.0))
+        vw0 = V(vec.memset(T.WT0[:, k + c:k + 16], -b / 4.0))
+    W("v", gset)
+    vj = V(vec.tensor_scalar(T.pm[:], T.pi[:], 15, None, Op.bitwise_and))
+    V(vec.memset(T.c130[0:32, :], 130.0))
+    V(vec.memset(T.XX[0:32, :], 0.0))
+    W("v", vj)
+    vj = V(vec.tensor_copy(T.pf[:], T.pm[:]))
+    for t in range(3):
+        V(vec.memset(T.kb[0:32, t:t + 1], 130.0 * HALF[t] - 0.125))
+    W("v", vj)
+    vj = V(vec.tensor_tensor(T.J[:], T.j0[:], T.pf[:], Op.add))
+    for b in range(1, n):
+        vset = V(vec.memset(T.WT0[64:128, 16 * (b - 1) + 4 * b - 3:16 * (b - 1) + 4 * b - 2], -b / 4.0))
     W("v", kw)
     vw = V(vec.quantize_mx(T.qw[:], T.qws[:], T.wt[:]))
 
-    def w_mm(k, b, C, Cs, a, m):
+    def w_mm(k, b, name, a, m):
         return P(ten.matmul_mx(bank(k, 0, m), T.qw[:, 128 * b:128 * b + 128], T.qws[:, 128 * b:128 * b + 128],
-                               C[:, a:a + m], Cs[:, a:a + m], True, True))
-
-    def own_mm(C, Cs, m, frees):
-        W("p", *frees)
-        return [w_mm(b, b, C, Cs, 0, m) for b in range(4)]
+                               T[name][:, a:a + m], T[name + "s"][:, a:a + m], True, True))
 
     def relu(q, out, src):
         if q == "a":
             return A(act.activation(out, src, Act.Relu, scale=0.0625))
         return V(vec.tensor_scalar(out, src, 0.0, 0.0625, Op.max, Op.mult))
 
-    def own_relu(pm, h, at, m):
+    def relus(q, bs, pm, k0, h, *runs):
         out = []
-        for b, q in ((0, "a"), (1, "v"), (2, "a"), (3, "v")):
+        for b in bs:
             W(q, pm[b])
-            out.append(relu(q, h[:, 4 * at + b:4 * (at + m):4], bank(b, 0, m)))
+            for a, c, m in runs:
+                out.append(relu(q, h[:, 4 * c + b:4 * (c + m):4], bank(k0 + b, a, a + m)))
         return out
 
-    pm = own_mm(T.C0, T.C0s, 256, [vx, vw])
-    W("v", V(vec.memset(T.zt[:], 0.0)))
+    W("p", vx, vw)
+    pm = [w_mm(b, b, "C0", 0, 256) for b in range(4)]
 
-    def zero_pads(t):
-        for a in ([48] if left is None else []) + [224 if right is not None else 176]:
-            out = V(vec.quantize_mx(T["N%d" % t][:, a:a + 128], T["N%ds" % t][:, a:a + 128], T.zt[:]))
-        return out
-    vpad = [zero_pads(0)]
-    rl = own_relu(pm, T.h1, 40, 256)
-    W("v", gset)
-    W("v", V(vec.tensor_scalar(T.pm[:], T.pi[:], 15, None, Op.bitwise_and)))
-    W("v", V(vec.tensor_copy(T.pf[:], T.pm[:])))
-    W("v", V(vec.tensor_tensor(T.J[:], T.j0[:], T.pf[:], Op.add)))
-    V(vec.tensor_copy(T.J8[:, 0:4], T.J[:, 0:4]))
-    V(vec.tensor_scalar(T.J8[:, 4:8], T.J[:, 0:4], -64.0, None, Op.add))
-    vpad += [zero_pads(1), zero_pads(2)]
-    V(vec.memset(T.hh1[:, 320:512], 0.0))
-    vh = V(vec.memset(T.hh2[:, 320:512], 0.0))
+    def zeros(name, *cols):
+        return [V(vec.quantize_mx(T[name][:, a:a + 128], T[name + "s"][:, a:a + 128], T.zt[:])) for a in cols]
+    pads = ([48] if left is None else []) + [224 if right is not None else 176]
+    V(vec.memset(T.h1[:, 0:160], 0.0))
+    V(vec.memset(T.h1[:, 1504:1536], 0.0))
+    vpad0 = zeros("N0", *pads)
+    rl = relus("a", (0, 2), pm, 0, T.h1, (0, 80, 256)) + relus("v", (1, 3), pm, 0, T.h1, (0, 80, 256))
+    W("v", *rl)
+    vq1 = V(vec.quantize_mx(T.W1[:, 128:256], T.W1s[:, 128:256], T.h1[:, 512:1024]))
+    W("p", *vpad0, a0, a1, ("nc0", n_in), ("ns0", n_in))
+    ph0 = [w_mm(4 + b, b, "N0", 128, 128) for b in range(4)]
+    W("p", vq1, *rl)
+    pc1 = cost_mm(0, "W1", 128)
 
-    def halo_mm(t, frees):
-        W("p", vpad[t], *frees)
-        W("p", ("nc%d" % t, n_in), ("ns%d" % t, n_in))
-        return [w_mm(4 + b, b, T["N%d" % t], T["N%ds" % t], 128, 128) for b in range(4)]
+    MW = (T.WT0, T.MW1, T.MW2)
+    BO = lambda t, a, b: T.BBB[:, 32 * t + a:32 * t + b]
 
-    def borders(t, own, act_mid, vec_mid):
-        Lt, Zq, Zh, Ih = T["L%d" % t], T["Zq%d" % t], T["Zh%d" % t], T["Ih%d" % t]
-        mo = 64 * t
-        rj = 256 * t
-        lm = ("lm%d" % t, l_in)
-        W("a", lm, vset, *own)
-        A(act.activation(T.MM[64:128, mo + 33:mo + 36], Lt[64:128, 3:12:4], Act.Copy))
-        ac = A(act.activation(T.MM[0:64, mo + 33:mo + 36], Lt[0:64, 7:16:4], Act.Copy))
-        W("v", lm, vset, *own)
-        for b in range(1, n):
-            vr = V(vec.tensor_reduce(T.MM[:, mo + b:mo + b + 1], Lt[:, b - 1:16:4], AxisListType.X, Op.add))
-        mids = act_mid()
-        W("v", vr)
+    def b_mult(t, *toks):
+        Lt = T["L%d" % t]
+        W("v", ("lm%d" % t, l_in), *toks)
+        for b in range(n - 1):
+            k = 48 * t + 16 * b
+            v = V(vec.tensor_tensor(T.LW[:, k:k + 16], Lt[:], MW[t][:, 16 * b:16 * b + 16], Op.mult))
+        if t:
+            v = V(vec.tensor_tensor(T.LM[:, 16 * t:16 * t + 16], Lt[:], T["MK%d" % t][:], Op.mult))
+        return v
+
+    def b_red(t, v):
+        mo = 96 * t
+        W("v", v, vmm)
+        for b in range(n - 1):
+            k = 48 * t + 16 * b
+            vq = V(vec.tensor_reduce(T.MM[:, mo + b + 1:mo + b + 2], T.LW[:, k:k + 16], AxisListType.X, Op.add))
+        vxx = vq
+        if t:
+            m = 16 * t
+            vxx = V(vec.tensor_tensor(T.MM[:, mo + 33:mo + 36], T.LM[:, m + 2:m + 11:4], T.LM[:, m + 4:m + 13:4], Op.add))
+            if t == 1:
+                vxx = V(vec.tensor_copy(T.MM[0:32, mo + 65:mo + 68], T.L1[0:32, 5:14:4]))
+            else:
+                vxx = V(vec.tensor_tensor(T.MM[:, mo + 65:mo + 68], T.LM[:, m + 3:m + 12:4], T.LM[:, m + 5:m + 14:4], Op.add))
+        return vq, vxx
+
+    def b_tq(t, vq):
+        mo = 96 * t
+        W("v", vq)
         for k in range(4):
-            vt = V(vec.transpose(Zq[0:32, 32 * k:32 * k + 32], T.MM[32 * k:32 * k + 32, mo:mo + 32]))
-        W("a", vt)
-        aq = A(act.activation(T.rjunk[0:5, rj:rj + 128], Zq[0:5, :], Act.Copy, accum_out=T.row[0:5, 4 + t:5 + t]))
-        W("v", ac)
+            v = V(vec.transpose(T["Zq%d" % t][0:32, 32 * k:32 * k + 32], T.MM[32 * k:32 * k + 32, mo:mo + 32]))
+        return v
+
+    def b_qsum(t, v):
+        W("a", v)
+        return A(act.activation(T.rjunk[0:5, 512 * t:512 * t + 128], T["Zq%d" % t][0:5, :], Act.Copy,
+                                accum_out=T["Ih%d" % t][0:5, 0:1]))
+
+    def b_tx(t, vxx):
+        mo, Zh = 96 * t + 32, T["Zh%d" % t]
+        W("v", vxx)
         for k in range(4):
-            z = (k + 2) % 4
-            vt = V(vec.transpose(Zh[0:32, 32 * z:32 * z + 32], T.MM[32 * k:32 * k + 32, mo + 32:mo + 64]))
-        W("v", vt)
-        vs = V(vec.tensor_tensor_scan(Ih[0:5, :], Zh[0:5, :], T.c130[0:5, :], 0.0, Op.add, Op.add))
-        W("v", vs, aq)
-        vb = V(vec.tensor_scalar(T.row[0:5, 7 + t:8 + t], Ih[0:5, 63:64], T.row[0:5, 4 + t:5 + t], T.row[0:5, t:t + 1],
-                                 Op.add, Op.add))
-        W("a", vb)
-        av = A(act.activation(T.rjunk[0:5, rj + 128:rj + 208], Ih[0:5, 23:103], Act.Sign, bias=T.row[0:5, 7 + t:8 + t],
-                              scale=-1.0, accum_out=T.row[0:5, 10 + t:11 + t]))
-        vm = vec_mid(mids)
-        W("v", av, gset)
-        W("v", V(vec.tensor_scalar(T.XX[0:5, 32 * t:32 * t + 32], T.nhb[0:5, :], T.row[0:5, 10 + t:11 + t], None, Op.mult)))
+            z = k if t else (k + 2) % 4
+            v = V(vec.transpose(Zh[0:32, 32 * z:32 * z + 32], T.MM[32 * k:32 * k + 32, mo:mo + 32]))
+        for k in range((0, 1, 4)[t]):
+            v = V(vec.transpose(Zh[0:32, 128 + 32 * k:160 + 32 * k], T.MM[32 * k:32 * k + 32, mo + 32:mo + 64]))
+        return v
+
+    def b_scan(t, v, aq):
+        h = 2 * HALF[t]
+        Ih = T["Ih%d" % t]
+        W("v", v, aq)
+        return V(vec.tensor_tensor_scan(Ih[0:5, 1:1 + h], T["Zh%d" % t][0:5, 0:h], T.c130[0:5, 0:h], Ih[0:5, 0:1], Op.add, Op.add))
+
+    def b_sign(t, v):
+        a, w = HALF[t] - MOVE[t], 2 * MOVE[t]
+        W("a", v)
+        return A(act.activation(T.rjunk[0:5, 512 * t + 128:512 * t + 128 + w], T["Ih%d" % t][0:5, a:a + w], Act.Sign,
+                                bias=T.kb[0:5, t:t + 1], scale=-1.0, accum_out=T.row[0:5, t:t + 1]))
+
+    def b_clamp(t, av):
+        X = T.XX[0:5, 32 * t:32 * t + 32]
+        W("v", av)
+        v = V(vec.tensor_scalar(X, T.lo[0:5, 32 * t:32 * t + 32], T.row[0:5, t:t + 1], T.hi[0:5, t:t + 1], Op.max, Op.min))
+        W("v", v)
         for k in range(4):
-            vB = V(vec.transpose(T.BBB[32 * k:32 * k + 32, 32 * t:32 * t + 32], T.XX[0:32, 32 * t:32 * t + 32]))
+            v = V(vec.transpose(T.BBB[32 * k:32 * k + 32, 32 * t:32 * t + 32], T.XX[0:32, 32 * t:32 * t + 32]))
         if t < 2:
-            V(vec.tensor_scalar(T.row[0:5, t + 1:t + 2], T.row[0:5, 10 + t:11 + t], -65.0, T.row[0:5, t:t + 1],
-                                Op.mult, Op.add))
-        W("v", vB)
-        vN = V(vec.tensor_tensor(T.Ball[:, 5 * t + 5:5 * t + 10], T.Ball[:, 5 * t:5 * t + 5],
-                                 T.BBB[:, 32 * t:32 * t + 5], Op.subtract))
-        return vm, vB, vN
+            V(vec.tensor_tensor(T.lo[0:5, 32 * t + 32:32 * t + 64], X, T.nhb[0:5, :], Op.subtract))
+            V(vec.tensor_tensor(T.hi[0:5, t + 1:t + 2], T.XX[0:5, 32 * t:32 * t + 1], T.nhb[0:5, 0:1], Op.add))
+        return v
 
-    Bl = lambda t: T.Ball[:, 5 * t + r:5 * t + r + 1]
-    Br = lambda t: T.Ball[:, 5 * t + r + 1:5 * t + r + 2]
-    el = lambda t: T.BBB[:, 32 * t + r:32 * t + r + 1]
-    er = lambda t: T.BBB[:, 32 * t + r + 1:32 * t + r + 2]
+    def b_masks(t, cols):
+        MK, MWt = T["MK%d" % t], MW[t]
+        for p, gc, is_left in cols:
+            if is_left:
+                v = V(vec.tensor_scalar(MK[:, p:16:4], BO(t - 1, 0, 4), T.gi[:, gc:gc + 1], None, Op.is_le))
+            else:
+                v = V(vec.tensor_scalar(MK[:, p:16:4], BO(t - 1, 1, 5), T.gi[:, gc:gc + 1], None, Op.is_gt))
+        W("v", v)
+        for b in range(n - 1):
+            v = V(vec.tensor_tensor(MWt[:, 16 * b:16 * b + 16], MK[:], T.WT1[:, 16 * b:16 * b + 16], Op.mult))
+        return v
 
-    def pick_ends(t, C, Cs, m, lst, vl, frees):
-        H, Hs = T["H%d" % t], T["H%ds" % t]
-        W("v", vl, *frees)
-        vp = V(vec.tensor_copy(H[:, 0:128].bitcast(dt.uint32), C[:, 0:m].bitcast(dt.uint32).indirect(lst[:, 0:8])))
-        W("a", vl, *frees)
-        ap = A(act.activation(Hs[:, 0:128], Cs[:, 0:m].indirect(lst[:, 0:8]), Act.Copy))
-        W("g", vp)
-        send_ends(t, H, "nc", 0, 80)
-        W("p", vp, ap)
-        ph = cost_mm(4, H, Hs, 0)
-        W("a", ph)
-        return ap, count(T["L%d" % t][:, 4 * r + 3:4 * r + 4], 4)
+    V(vec.tensor_scalar(T.lo[0:32, 0:32], T.nhb[0:32, :], -1.0, None, Op.mult))
+    V(vec.tensor_copy(T.hi[0:32, 0:1], T.nhb[0:32, 0:1]))
+    W("a", ("lm0", l_in), vmm, a0, a1)
+    A(act.activation(T.MM[64:128, 33:36], T.L0[64:128, 1:10:4], Act.Copy))
+    ax = A(act.activation(T.MM[0:64, 33:36], T.L0[0:64, 4:13:4], Act.Copy))
+    vm = b_mult(0, vset, a0, a1)
+    vq, _ = b_red(0, vm)
+    vt = b_tq(0, vq)
+    vt2 = b_tx(0, ax)
+    aq = b_qsum(0, vt)
+    halo = ((8, 40, 40), (48, 336, 40))
+    hr = relus("a", (0, 2), ph0, 4, T.h1, *halo)
+    hr += relus("v", (1, 3), ph0, 4, T.h1, *halo)
+    ac1 = count(1, 1, 0, pc1)
+    vs = b_scan(0, vt2, aq)
+    W("v", *hr, *rl)
+    vp0 = V(vec.quantize_mx(T.W1[:, 0:128], T.W1s[:, 0:128], T.h1[:, 0:512]))
+    vp2 = V(vec.quantize_mx(T.W1[:, 256:384], T.W1s[:, 256:384], T.h1[:, 1024:1536]))
+    av = b_sign(0, vs)
+    W("p", vp0)
+    pc0 = cost_mm(1, "W1", 0)
+    W("p", vp2)
+    pc2 = cost_mm(2, "W1", 256)
+    ac0 = count(1, 0, 1, pc0)
+    ac2 = count(1, 2, 2, pc2)
+    W("g", vp2)
+    send_ends(1, "nc", "W1", "W1", 120, (40, 512), (256, 384))
+    send_ends(1, "ns", "W1", "W1", 120, (40, 512), (256, 384))
+    W("g", ac0, ac1, ac2)
+    send_costs(1)
+    W("p", *rl, ac0, ac1, ac2)
+    pm = [w_mm(b, b, "W1", 128, 160) for b in range(4)]
+    W("v", vj)
+    V(vec.tensor_scalar(T.JL[:], T.J[:, 0:8], 2.0, -160.0, Op.mult, Op.add))
+    V(vec.tensor_scalar(T.JR[:], T.J[:, 0:8], 2.0, -96.0, Op.mult, Op.add))
+    V(vec.tensor_copy(T.Jm[:, 0:8], T.J[:, 0:8]))
+    vj = V(vec.tensor_scalar(T.Jm[:, 8:16], T.J[:, 0:8], 288.0, None, Op.add))
+    vB = b_clamp(0, av)
+    W("v", vB, vj)
+    V(vec.tensor_scalar(T.t1[:, 0:8], T.JL[:], BO(0, r, r + 1), 384.0, Op.is_lt, Op.mult))
+    vl = V(vec.tensor_scalar(T.t1[:, 8:16], T.JR[:], BO(0, r + 1, r + 2), 216.0, Op.is_ge, Op.mult))
+    V(vec.memset(T.m2[:, 0:160], 0.0))
+    W("v", vl)
+    vl = V(vec.tensor_tensor(T.t2[:], T.t1[:], T.Jm[:], Op.add))
+    V(vec.memset(T.m2[:, 1824:2048], 0.0))
+    W("v", vl)
+    vl = V(vec.tensor_copy(T.la[:], T.t2[:]))
+    rm = relus("a", (0, 2), pm, 0, T.m2, (0, 168, 160)) + relus("v", (1, 3), pm, 0, T.m2, (0, 168, 160))
+    mk1 = b_masks(1, ((0, 0, True), (2, 0, False)))
+    vpad1 = zeros("W1", *(([384] if left is None else []) + ([512] if right is None else [])))
+    vpad2 = zeros("N2", *pads)
 
-    def finish_costs(t, vtile, k, toks, ap, ac):
-        W("v", *toks)
-        W("v", V(vec.tensor_reduce(T.par[:, t:t + 1], vtile[:, 0:k], AxisListType.X, Op.add)))
-        vq = V(vec.tensor_scalar(T["L%d" % t][:, 4 * r:4 * r + 3], T.wts[:, 0:3], T.par[:, t:t + 1], None, Op.mult))
-        W("g", vq, ac)
-        send_costs(t)
-        W("g", ap)
-        send_ends(t, T["H%ds" % t], "ns", 0, 80)
-        return [vq, ac]
+    vpk, apk = [], []
+    W("v", vl, vp2, vq1, *vpad1, ("nc1", n_in))
+    W("a", vl, vp2, vq1, *vpad1, ("ns1", n_in))
+    for k in (0, 1):
+        s = slice(128 * k, 128 * k + 128)
+        l = T.la[:, 8 * k:8 * k + 8]
+        vpk.append(V(vec.tensor_copy(T.M1[:, s].bitcast(dt.uint32), T.W1[:, 0:640].bitcast(dt.uint32).indirect(l))))
+        apk.append(A(act.activation(T.M1s[:, s], T.W1s[:, 0:640].indirect(l), Act.Copy)))
+    W("p", vpk[0], apk[0], *hr)
+    pL = [w_mm(4 + b, b, "M1", 0, 128) for b in range(4)]
+    W("p", vpk[1], apk[1], *rm)
+    pR = [w_mm(b, b, "M1", 128, 128) for b in range(4)]
+    vm = b_mult(1, mk1, ac0, ac1, ac2)
+    rL = relus("a", (0, 2), pL, 4, T.m2, (0, 40, 128)) + relus("v", (1,), pL, 4, T.m2, (0, 40, 128))
+    vq, vxx = b_red(1, vm)
+    rL += relus("v", (3,), pL, 4, T.m2, (0, 40, 128))
+    vt = b_tq(1, vq)
+    W("v", *rL, *rm)
+    vc0 = V(vec.quantize_mx(T.C2[:, 0:256], T.C2s[:, 0:256], T.m2[:, 0:1024]))
+    rR = relus("a", (0,), pR, 0, T.m2, (0, 328, 128))
+    aq = b_qsum(1, vt)
+    rR += relus("a", (2,), pR, 0, T.m2, (0, 328, 128)) + relus("v", (1, 3), pR, 0, T.m2, (0, 328, 128))
+    vt2 = b_tx(1, vxx)
+    W("v", *rR)
+    vc1 = V(vec.quantize_mx(T.C2[:, 256:512], T.C2s[:, 256:512], T.m2[:, 1024:2048]))
+    vs = b_scan(1, vt2, aq)
+    W("p", vc0, *rL)
+    pc = [cost_mm(4, "C2", 0), cost_mm(5, "C2", 128)]
+    W("p", vc1)
+    pc += [cost_mm(6, "C2", 256), cost_mm(7, "C2", 384)]
+    ac = [count(2, k, 4 + k, pc[k]) for k in range(4)]
+    av = b_sign(1, vs)
+    W("g", *ac)
+    send_costs(2)
+    W("p", *rR)
+    pm = [w_mm(b, b, "C2", 40, 416) for b in range(4)]
+    ro = relus("a", (0,), pm, 0, T.m3, (0, 0, 416))
+    V(vec.tensor_scalar(T.J8[:, 0:4], T.J[:, 0:4], 2.0, 240.0, Op.mult, Op.add))
+    vj = V(vec.tensor_scalar(T.J8[:, 4:8], T.J[:, 0:4], 2.0, 624.0, Op.mult, Op.add))
+    V(vec.tensor_scalar(T.J2[:], T.J[:], 2.0, None, Op.mult))
+    V(vec.tensor_scalar(T.J2m[:], T.J[:], 2.0, -512.0, Op.mult, Op.add))
+    vz = V(vec.memset(T.hh2[:, 320:512], 0.0))
+    vB = b_clamp(1, av)
+    W("v", vB, vj)
+    V(vec.tensor_scalar(T.lb[:, 0:4], T.J8[:, 0:4], BO(1, r, r + 1), 0.5, Op.add, Op.mult))
+    vl = V(vec.tensor_scalar(T.lb[:, 4:8], T.J8[:, 4:8], BO(1, r + 1, r + 2), 0.5, Op.add, Op.mult))
+    W("v", vl)
+    vh = V(vec.tensor_copy(T.H2[:].bitcast(dt.uint32), T.C2[:, 0:512].bitcast(dt.uint32).indirect(T.lb[:, 0:8])))
+    W("a", vl, vc1)
+    ah = A(act.activation(T.H2s[:], T.C2s[:, 0:512].indirect(T.lb[:, 0:8]), Act.Copy))
+    W("g", vh)
+    send_ends(2, "nc", "H2", "N2", 48, (0, 176), (80, 128))
+    W("g", ah)
+    send_ends(2, "ns", "H2", "N2", 48, (0, 176), (80, 128))
+    mk2 = b_masks(2, ((0, 1, True), (1, 2, True), (2, 1, False), (3, 2, False)))
+    V(vec.tensor_scalar(T.kk[:, 0:1], BO(1, r, r + 1), -0.5, 376.0, Op.mult, Op.add))
+    vk = V(vec.tensor_scalar(T.kk[:, 1:2], BO(1, r + 1, r + 2), -0.5, 120.0, Op.mult, Op.add))
 
-    ph0 = halo_mm(0, [a0, a1])
+    def bd_row(t):
+        W("v", V(vec.tensor_scalar(T.Bh[:, 5 * t:5 * t + 5], BO(t, 0, 5), 0.5, None, Op.mult)))
+        return V(vec.tensor_tensor(T.Ball[:, 5 * t:5 * t + 5], T.Bh[:, 5 * t:5 * t + 5], T.B0[:], Op.add))
 
-    def mid0():
-        out = []
-        for b in range(4):
-            W("a", ph0[b])
-            out.append(relu("a", T.h1[:, b:160:4], bank(4 + b, 8, 48)))
-            out.append(relu("a", T.h1[:, 1184 + b:1344:4], bank(4 + b, 48, 88)))
-        return out
-
-    def q1(mids):
-        W("v", *mids, *rl)
-        return V(vec.quantize_mx(T.C1[:], T.C1s[:], T.h1[:]))
-    vm, vB, vN = borders(0, own, mid0, q1)
-    W("p", vm)
-    pc = [cost_mm(k, T.C1, T.C1s, a) for k, a in enumerate((0, 128, 208))]
-    ac = []
-    for k, out in enumerate((T.cc[:, 2:3], T.va[:, 1:2], T.cc[:, 3:4])):
-        W("a", pc[k])
-        ac.append(count(out, k))
-    V(vec.tensor_scalar(T.la[:, 0:4], T.J8[:, 0:4], el(0), 40.0, Op.subtract, Op.add))
-    vl = V(vec.tensor_scalar(T.la[:, 4:8], T.J8[:, 4:8], er(0), 296.0, Op.subtract, Op.add))
-    ap, ach = pick_ends(1, T.C1, T.C1s, 336, T.la, vl, [vm])
-    W("v", vN, *ac)
-    V(vec.tensor_scalar(T.va[:, 0:1], T.gi[:, 0:1], Bl(1), T.cc[:, 2:3], Op.is_ge, Op.mult))
-    vv = V(vec.tensor_scalar(T.va[:, 2:3], T.gx[:, 2:3], Br(1), T.cc[:, 3:4], Op.is_lt, Op.mult))
-    own = finish_costs(1, T.va, 3, [vv], ap, ach)
-
-    pm = own_mm(T.C1, T.C1s, 336, [vm, *ac])
-    rl = own_relu(pm, T.m2, 0, 336)
-    W("v", *rl)
-    vc2 = V(vec.quantize_mx(T.C2[:, 0:336], T.C2s[:, 0:336], T.m2[:]))
-    vk1 = V(vec.tensor_scalar(T.kk[:, 0:2], T.Ball[:, 5 + r:7 + r], -1.0, float(336 + base), Op.mult, Op.add))
-    W("p", vc2)
-    pc = [cost_mm(k, T.C2, T.C2s, a) for k, a in enumerate((0, 128, 208))]
-    ac = []
-    for k in range(3):
-        W("a", pc[k])
-        ac.append(count(T.cc[:, 4 + k:5 + k], k))
-    ph1 = halo_mm(1, [ach])
-
-    def halo_relus(ph, hh):
-        def f():
-            out = []
-            for b in range(4):
-                W("a", ph[b])
-                out.append(relu("a", hh[:, b:320:4], bank(4 + b, 8, 88)))
-            return out
-        return f
-
-    def q2(mids):
-        W("v", vh, *mids)
-        return V(vec.quantize_mx(T.C2[:, 336:464], T.C2s[:, 336:464], T.hh1[:]))
-    vm, vB, vN = borders(1, own, halo_relus(ph1, T.hh1), q2)
-    W("p", vm)
-    ppc = cost_mm(3, T.C2, T.C2s, 336)
-    W("a", ppc)
-    ac.append(count(T.cc[:, 7:8], 3))
-    W("v", vB, vk1)
-    V(vec.tensor_scalar(T.t8[:, 0:4], T.J8[:, 0:4], el(1), T.kk[:, 0:1], Op.is_lt, Op.mult))
-    W("v", V(vec.tensor_scalar(T.t8[:, 4:8], T.J8[:, 4:8], er(1), T.kk[:, 1:2], Op.is_ge, Op.mult)))
-    W("v", V(vec.tensor_tensor(T.t9[:], T.t8[:], T.J8[:], Op.add)), vN)
-    V(vec.tensor_scalar(T.lb[:, 0:4], T.t9[:, 0:4], Bl(2), float(40 - base), Op.add, Op.add))
-    vl = V(vec.tensor_scalar(T.lb[:, 4:8], T.t9[:, 4:8], Br(2), float(40 - base), Op.add, Op.add))
-    ap, ach = pick_ends(2, T.C2, T.C2s, 416, T.lb, vl, [vm, vc2])
-    V(vec.tensor_tensor(T.kk[:, 4:5], Bl(1), Bl(2), Op.max))
-    v1 = V(vec.tensor_tensor(T.kk[:, 5:6], Br(1), Br(2), Op.min))
-    W("v", *ac)
-    V(vec.tensor_scalar(T.vb[:, 3:4], T.gx[:, 3:4], el(1), T.cc[:, 7:8], Op.is_le, Op.mult))
-    V(vec.tensor_scalar(T.vb[:, 4:5], T.gx[:, 4:5], er(1), T.cc[:, 7:8], Op.is_gt, Op.mult))
-    W("v", v1)
-    V(vec.tensor_scalar(T.vb[:, 0:1], T.gi[:, 0:1], T.kk[:, 4:5], T.cc[:, 4:5], Op.is_ge, Op.mult))
-    V(vec.tensor_scalar(T.vb[:, 1:2], T.gi[:, 1:2], T.kk[:, 5:6], T.cc[:, 5:6], Op.is_lt, Op.mult))
-    vv = V(vec.tensor_scalar(T.vb[:, 2:3], T.gx[:, 2:3], T.kk[:, 5:6], T.cc[:, 6:7], Op.is_lt, Op.mult))
-    own = finish_costs(2, T.vb, 5, [vv], ap, ach)
-
-    pm = own_mm(T.C2, T.C2s, 416, [vm, vc2, *ac])
-    W("v", V(vec.tensor_scalar(T.kk[:, 2:4], T.Ball[:, 10 + r:12 + r], -1.0, float(416 + base), Op.mult, Op.add)))
-    vk3 = V(vec.tensor_tensor(T.kk[:, 6:8], T.kk[:, 2:4], T.kk[:, 0:2], Op.subtract))
-    rl = own_relu(pm, T.m3, 0, 416)
-    W("v", *rl)
+    ro += relus("a", (2,), pm, 0, T.m3, (0, 0, 416)) + relus("v", (1,), pm, 0, T.m3, (0, 0, 416))
+    vm = b_mult(2, mk2, *ac)
+    vq, vxx = b_red(2, vm)
+    vt = b_tq(2, vq)
+    vt2 = b_tx(2, vxx)
+    aq = b_qsum(2, vt)
+    ro += relus("a", (3,), pm, 0, T.m3, (0, 0, 416))
+    vs = b_scan(2, vt2, aq)
+    av = b_sign(2, vs)
+    W("p", *vpad2, *ac, ("nc2", n_in), ("ns2", n_in))
+    ph = [w_mm(4 + b, b, "N2", 128, 128) for b in range(4)]
+    W("v", *ro)
     vc3 = V(vec.quantize_mx(T.C3[:, 0:416], T.C3s[:, 0:416], T.m3[:]))
-    ph2 = halo_mm(2, [ach])
-
-    def q3(mids):
-        W("v", vh, *mids)
-        return V(vec.quantize_mx(T.C3[:, 416:544], T.C3s[:, 416:544], T.hh2[:]))
-    vm, vB, vN = borders(2, own, halo_relus(ph2, T.hh2), q3)
-    W("v", vN)
-    U = T.terms[:, 0:31]
-    W("v", V(vec.tensor_scalar(U, T.J[:], Bl(3), None, Op.add)), vk3)
-    V(vec.tensor_scalar(T.terms[:, 31:62], U, Bl(2), T.kk[:, 6:7], Op.is_lt, Op.mult))
-    V(vec.tensor_scalar(T.terms[:, 62:93], U, T.kk[:, 4:5], T.kk[:, 0:1], Op.is_lt, Op.mult))
-    V(vec.tensor_scalar(T.terms[:, 93:124], U, Br(2), T.kk[:, 7:8], Op.is_ge, Op.mult))
-    V(vec.tensor_scalar(T.terms[:, 124:155], U, T.kk[:, 5:6], T.kk[:, 1:2], Op.is_ge, Op.mult))
-    W("v", V(vec.tensor_scalar(T.terms[:, 155:186], U, Br(3), 2000.0, Op.is_ge, Op.mult)))
-    W("v", V(vec.tensor_tensor(T.sum3[:, 0:93], T.terms[:, 0:93], T.terms[:, 93:186], Op.add)))
-    W("v", V(vec.tensor_tensor(T.sum2[:, 0:31], T.sum3[:, 0:31], T.sum3[:, 31:62], Op.add)))
-    W("v", V(vec.tensor_tensor(T.sum1[:, 0:31], T.sum2[:, 0:31], T.sum3[:, 62:93], Op.add)))
-    vl = V(vec.tensor_scalar(T.lf[:, 0:31], T.sum1[:, 0:31], float(40 - base), 500.0, Op.add, Op.min))
-    W("s", vN)
-    inc("dout", g.sync.dma_start(T.bd[:], T.Ball[0:1, 5:20]), 16)
-    W("v", vl, vm, vc3)
-    W("a", vl, vm, vc3)
+    h2 = relus("a", (0, 2), ph, 4, T.hh2, (8, 0, 80))
+    vB = b_clamp(2, av)
+    h2 += relus("v", (1, 3), ph, 4, T.hh2, (8, 0, 80))
+    W("v", vB, vk)
+    U2, V2, U = T.terms[:, 0:31], T.terms[:, 31:62], T.terms[:, 62:93]
+    V(vec.tensor_scalar(U2, T.J2[:], BO(2, r, r + 1), None, Op.add))
+    V(vec.tensor_scalar(V2, T.J2m[:], BO(2, r, r + 1), None, Op.add))
+    vu = V(vec.tensor_scalar(U, T.J2[:], BO(2, r, r + 1), 0.5, Op.add, Op.mult))
+    W("v", vz, *h2)
+    vch = V(vec.quantize_mx(T.C3[:, 416:544], T.C3s[:, 416:544], T.hh2[:]))
+    W("v", vu)
+    V(vec.tensor_scalar(T.terms[:, 93:124], U2, BO(1, r, r + 1), T.kk[:, 0:1], Op.is_lt, Op.mult))
+    V(vec.tensor_scalar(T.terms[:, 124:155], V2, BO(1, r + 1, r + 2), T.kk[:, 1:2], Op.is_ge, Op.mult))
+    vu = V(vec.tensor_scalar(T.terms[:, 155:186], V2, BO(2, r + 1, r + 2), 2000.0, Op.is_ge, Op.mult))
+    W("v", vu)
+    vu = V(vec.tensor_tensor(T.sum3[:, 0:62], T.terms[:, 62:124], T.terms[:, 124:186], Op.add))
+    W("v", vu)
+    vu = V(vec.tensor_tensor(T.sum1[:, 0:31], T.sum3[:, 0:31], T.sum3[:, 31:62], Op.add))
+    W("v", vu)
+    vl = V(vec.tensor_scalar(T.lf[:, 0:31], T.sum1[:, 0:31], 80.0, 500.0, Op.add, Op.min))
+    W("v", vl, vch, vc3)
+    W("a", vl, vch, vc3)
     halves = (("FA", 0, 256), ("FB", 256, 496))
     vf, af, py = [], [], []
     for F, a, b in halves:
         l = T.lf[:, a // 16:b // 16]
         vf.append(V(vec.tensor_copy(T[F][:].bitcast(dt.uint32), T.C3[:, 0:544].bitcast(dt.uint32).indirect(l))))
         af.append(A(act.activation(T[F + "s"][:], T.C3s[:, 0:544].indirect(l), Act.Copy)))
+    W("p", *ro)
     for k, (F, a, b) in enumerate(halves):
         W("p", vf[k], af[k])
         py.append(P(ten.matmul_mx(bank(k, 0, b - a), T.qa[:], T.qas[:], T[F][:], T[F + "s"][:], True, True)))
+    bd_row(0)
+    bd_row(1)
+    vN = bd_row(2)
     W("v", py[0])
     vy = V(vec.tensor_copy(T.yt[:, 0:256], bank(0, 0, 256)))
     W("a", py[1])
@@ -402,6 +470,8 @@ def rank_program(g, core, T, topo):
     out_codes(0)
     out_scales("s", 0)
     out_codes(1)
+    W("s", vN)
+    inc("dout", g.sync.dma_start(T.bd[:], T.Ball[0:1, 0:15]), 16)
     W("s", vy)
     inc("dout", g.sync.dma_start(T.y[:, 0:256], T.yt[:, 0:256]), 16)
     W("a", ay)

@@ -4,16 +4,16 @@ from concourse.mybir import dt, AluOpType as Op, AxisListType, ActivationFunctio
 
 F32, BF, I32, U16, F8, U8 = "float32", "bfloat16", "int32", "uint16", "float8_e4m3fn_x4", "uint8"
 SCRATCH = {"ps": ("psum", [128, 4096], F32)}
-for _names, _d in (("xt:1024 at:512 wt:2048 h1:1536 m2:2048 m3:1664 hh2:512 zt:512 junk:1280", BF),
-                   ("eps:4 kb:4 c130:256 nh:32 nha:32 nhb:32 MM:288 XX:96 lo:96 hi:4 BBB:96 row:16 rjunk:1536 B0:5 Bh:16 Ball:16 "
-                    "pf:31 j0:31 J:31 J2:31 J2m:31 JL:8 JR:8 Jm:16 J8:8 gi:4 WT0:48 WT1:48 MK1:16 MK2:16 MW1:48 MW2:48 "
-                    "LW:144 LM:48 t1:16 t2:16 kk:4 terms:192 sum3:64 sum1:32 yt:496 L0:16 L1:16 L2:16 "
+for _names, _d in (("xt:1024 at:512 wt:2048 h1:1536 m2:2048 m3:1664 hh2:512 zt:512 junk:1408", BF),
+                   ("eps:4 kb:4 c130:256 nh:32 nha:32 nhb:32 MM:288 XX:96 lo:96 hi:4 BBB:96 row:16 rjunk:1536 B0:15 Bh:16 Ball:16 "
+                    "pf:31 j0:31 J:31 J2:31 J2m:31 JL:8 JR:8 Jm:16 J8:8 gi:4 wq:4 z16:16 WT:48 MW:48 LW:48 MK1:16 MK2:16 "
+                    "LM:48 PS:48 TW:16 t1:16 t2:16 kk:4 terms:192 sum3:64 sum1:32 yt:512 YC:544 L0:16 L1:16 L2:16 "
                     "Zq0:128 Zq1:128 Zq2:128 Zh0:128 Zh1:160 Zh2:256 Ih0:132 Ih1:164 Ih2:244", F32),
                    ("pi:31 pm:31", I32), ("la:16 lb:8 lf:32", U16)):
     for _s in _names.split():
         SCRATCH[_s.split(":")[0]] = ("sbuf", [128, int(_s.split(":")[1])], _d)
 for _n, _w in (("qa", 128), ("qw", 512), ("C0", 256), ("W1", 640), ("M1", 256), ("C2", 512), ("C3", 544), ("H2", 128),
-               ("N0", 352), ("N2", 352), ("FA", 256), ("FB", 240)):
+               ("N0", 352), ("N2", 352), ("F", 496)):
     SCRATCH[_n] = ("sbuf", [128, _w], F8)
     SCRATCH[_n + "s"] = ("sbuf", [128, _w], U8)
 SEMAPHORES = ["sv", "sa", "sp", "gc", "dx0", "dx1", "da", "dw", "dout", "ls"] + \
@@ -98,18 +98,23 @@ def rank_program(g, core, T, topo):
     inc("dw", act.dma_start(T.wt[:, 1024:2048], T.w[:, 1024:2048]), 16)
     kw = inc("dw", g.sync.dma_start(T.wt[:, 0:1024], T.w[:, 0:1024]), 16)
 
+    def zeros(name, *cols):
+        return [V(vec.quantize_mx(T[name][:, a:a + 128], T[name + "s"][:, a:a + 128], T.zt[:])) for a in cols]
+    pads = ([48] if left is None else []) + [224 if right is not None else 176]
     vnh = V(vec.memset(T.nh[0:32, :], 80.0))
+    vz = V(vec.memset(T.zt[:], 0.0))
     for t in range(3):
         V(vec.memset(T["L%d" % t][:, 4 * r:4 * r + 4], 0.0))
     veps = V(vec.memset(T.eps[:, 0:1], -(2.0 ** -120)))
     for b in range(1, n):
         k, c = 16 * (b - 1), 4 * (b - 1) + 2
-        V(vec.memset(T.WT1[:, k:k + c], 1 - b / 4.0))
-        V(vec.memset(T.WT1[:, k + c:k + 16], -b / 4.0))
-    V(vec.memset(T.MK1[:], 1.0))
+        V(vec.memset(T.WT[:, k:k + c], 1 - b / 4.0))
+        V(vec.memset(T.WT[:, k + c:k + 16], -b / 4.0))
+    W("v", vz)
+    vpad0 = zeros("N0", *pads)
     G(g.iota(T.pi[:], [[0, 31]], 0, 1))
     G(g.iota(T.j0[:], [[16, 31]], 0, 0, allow_small_or_imprecise_dtypes=True))
-    G(g.iota(T.B0[:], [[256, 5]], 0, 0, allow_small_or_imprecise_dtypes=True))
+    G(g.iota(T.B0[:], [[0, 3], [256, 5]], 0, 0, allow_small_or_imprecise_dtypes=True))
     for k, b0 in enumerate((-160, -240, 16)):
         G(g.iota(T.gi[:, k:k + 1], [[0, 1]], b0, 2, allow_small_or_imprecise_dtypes=True))
     W("g", vnh)
@@ -125,47 +130,34 @@ def rank_program(g, core, T, topo):
     va = V(vec.quantize_mx(T.qa[:], T.qas[:], T.at[:]))
     W("g", vx)
     send_ends(0, "nc", "C0", "N0", 48, (0, 176), (208, 128))
+    send_ends(0, "ns", "C0", "N0", 48, (0, 176), (208, 128))
 
     def cost_mm(k, name, a):
         return P(ten.matmul_mx(bank(k, 0, 128), T[name][:, a:a + 128], T[name + "s"][:, a:a + 128], T.qa[:], T.qas[:], True, True))
 
     junk = []
 
-    def count(t, piece, k, tok):
+    def count(t, piece, k, tok, a=0, b=128):
         W("a", tok)
         j = 128 * len(junk)
         junk.append(j)
         c = 4 * r + piece
-        return A(act.activation(T.junk[:, j:j + 128], bank(k, 0, 128), Act.Sign, bias=T.eps[:, 0:1],
-                                accum_out=T["L%d" % t][:, c:c + 1]))
+        return A(act.activation(T.junk[a:b, j:j + 128], T.ps[a:b, 512 * k:512 * k + 128], Act.Sign, bias=T.eps[a:b, 0:1],
+                                accum_out=T["L%d" % t][a:b, c:c + 1]))
 
     W("p", va)
     p0, p1 = cost_mm(4, "C0", 0), cost_mm(5, "C0", 128)
     W("a", veps)
-    a0 = count(0, 0, 4, p0)
-    a1 = count(0, 1, 5, p1)
+    count(0, 0, 4, p0)
+    count(0, 1, 5, p1, 0, 64)
+    a1 = count(0, 2, 5, p1, 64, 128)
     W("g", a1)
     send_costs(0)
-    send_ends(0, "ns", "C0", "N0", 48, (0, 176), (208, 128))
 
+    V(vec.memset(T.h1[:, 0:160], 0.0))
+    V(vec.memset(T.h1[:, 1504:1536], 0.0))
     vmm = V(vec.memset(T.MM[:], 0.0))
-    V(vec.memset(T.zt[:], 0.0))
-    for b in range(1, n):
-        k, c = 16 * (b - 1), 4 * (b - 1) + 2
-        V(vec.memset(T.WT0[:, k:k + c], 1 - b / 4.0))
-        vw0 = V(vec.memset(T.WT0[:, k + c:k + 16], -b / 4.0))
-    W("v", gset)
-    vj = V(vec.tensor_scalar(T.pm[:], T.pi[:], 15, None, Op.bitwise_and))
-    V(vec.memset(T.c130[0:32, :], 130.0))
     V(vec.memset(T.XX[0:32, :], 0.0))
-    W("v", vj)
-    vj = V(vec.tensor_copy(T.pf[:], T.pm[:]))
-    for t in range(3):
-        V(vec.memset(T.kb[0:32, t:t + 1], 130.0 * HALF[t] - 0.125))
-    W("v", vj)
-    vj = V(vec.tensor_tensor(T.J[:], T.j0[:], T.pf[:], Op.add))
-    for b in range(1, n):
-        vset = V(vec.memset(T.WT0[64:128, 16 * (b - 1) + 4 * b - 3:16 * (b - 1) + 4 * b - 2], -b / 4.0))
     W("v", kw)
     vw = V(vec.quantize_mx(T.qw[:], T.qws[:], T.wt[:]))
 
@@ -188,49 +180,46 @@ def rank_program(g, core, T, topo):
 
     W("p", vx, vw)
     pm = [w_mm(b, b, "C0", 0, 256) for b in range(4)]
-
-    def zeros(name, *cols):
-        return [V(vec.quantize_mx(T[name][:, a:a + 128], T[name + "s"][:, a:a + 128], T.zt[:])) for a in cols]
-    pads = ([48] if left is None else []) + [224 if right is not None else 176]
-    V(vec.memset(T.h1[:, 0:160], 0.0))
-    V(vec.memset(T.h1[:, 1504:1536], 0.0))
-    vpad0 = zeros("N0", *pads)
+    V(vec.memset(T.z16[:], 0.0))
+    for b in range(1, n):
+        V(vec.memset(T.wq[:, b - 1:b], b / 4.0))
+    V(vec.memset(T.c130[0:32, :], 130.0))
     rl = relus("a", (0, 2), pm, 0, T.h1, (0, 80, 256)) + relus("v", (1, 3), pm, 0, T.h1, (0, 80, 256))
     W("v", *rl)
     vq1 = V(vec.quantize_mx(T.W1[:, 128:256], T.W1s[:, 128:256], T.h1[:, 512:1024]))
-    W("p", *vpad0, a0, a1, ("nc0", n_in), ("ns0", n_in))
+    for t in range(3):
+        V(vec.memset(T.kb[0:32, t:t + 1], 130.0 * HALF[t] - 0.125))
+    W("p", *vpad0, a1, ("nc0", n_in), ("ns0", n_in))
     ph0 = [w_mm(4 + b, b, "N0", 128, 128) for b in range(4)]
     W("p", vq1, *rl)
     pc1 = cost_mm(0, "W1", 128)
 
-    MW = (T.WT0, T.MW1, T.MW2)
     BO = lambda t, a, b: T.BBB[:, 32 * t + a:32 * t + b]
 
-    def b_mult(t, *toks):
-        Lt = T["L%d" % t]
+    def b_mask(t, *toks):
         W("v", ("lm%d" % t, l_in), *toks)
-        for b in range(n - 1):
-            k = 48 * t + 16 * b
-            v = V(vec.tensor_tensor(T.LW[:, k:k + 16], Lt[:], MW[t][:, 16 * b:16 * b + 16], Op.mult))
-        if t:
-            v = V(vec.tensor_tensor(T.LM[:, 16 * t:16 * t + 16], Lt[:], T["MK%d" % t][:], Op.mult))
-        return v
+        return V(vec.tensor_tensor(T.LM[:, 16 * t:16 * t + 16], T["L%d" % t][:], T["MK%d" % t][:], Op.mult))
 
-    def b_red(t, v):
-        mo = 96 * t
-        W("v", v, vmm)
-        for b in range(n - 1):
-            k = 48 * t + 16 * b
-            vq = V(vec.tensor_reduce(T.MM[:, mo + b + 1:mo + b + 2], T.LW[:, k:k + 16], AxisListType.X, Op.add))
-        vxx = vq
-        if t:
-            m = 16 * t
-            vxx = V(vec.tensor_tensor(T.MM[:, mo + 33:mo + 36], T.LM[:, m + 2:m + 11:4], T.LM[:, m + 4:m + 13:4], Op.add))
-            if t == 1:
-                vxx = V(vec.tensor_copy(T.MM[0:32, mo + 65:mo + 68], T.L1[0:32, 5:14:4]))
-            else:
-                vxx = V(vec.tensor_tensor(T.MM[:, mo + 65:mo + 68], T.LM[:, m + 3:m + 12:4], T.LM[:, m + 5:m + 14:4], Op.add))
-        return vq, vxx
+    def b_ps(t, *toks):
+        W("v", *toks)
+        src = T.LM[:, 16 * t:16 * t + 16] if t else T.L0[:]
+        return V(vec.tensor_tensor_scan(T.PS[:, 16 * t:16 * t + 16], src, T.z16[:], 0.0, Op.add, Op.add))
+
+    def b_x(t):
+        m, mo = 16 * t, 96 * t
+        v = V(vec.tensor_tensor(T.MM[:, mo + 33:mo + 36], T.LM[:, m + 2:m + 11:4], T.LM[:, m + 4:m + 13:4], Op.add))
+        if t == 1:
+            return V(vec.tensor_copy(T.MM[0:32, mo + 65:mo + 68], T.L1[0:32, 5:14:4]))
+        return V(vec.tensor_tensor(T.MM[:, mo + 65:mo + 68], T.LM[:, m + 3:m + 12:4], T.LM[:, m + 5:m + 14:4], Op.add))
+
+    def b_share(t, v):
+        W("v", v)
+        return V(vec.tensor_scalar(T.TW[:, 4 * t:4 * t + 3], T.wq[:, 0:3], T.PS[:, 16 * t + 15:16 * t + 16], None, Op.mult))
+
+    def b_sub(t, v):
+        W("v", v)
+        return V(vec.tensor_tensor(T.MM[:, 96 * t + 1:96 * t + 4], T.PS[:, 16 * t + 1:16 * t + 10:4], T.TW[:, 4 * t:4 * t + 3],
+                                   Op.subtract))
 
     def b_tq(t, vq):
         mo = 96 * t
@@ -244,14 +233,16 @@ def rank_program(g, core, T, topo):
         return A(act.activation(T.rjunk[0:5, 512 * t:512 * t + 128], T["Zq%d" % t][0:5, :], Act.Copy,
                                 accum_out=T["Ih%d" % t][0:5, 0:1]))
 
-    def b_tx(t, vxx):
+    def b_tx(t, vxx, half):
         mo, Zh = 96 * t + 32, T["Zh%d" % t]
         W("v", vxx)
-        for k in range(4):
-            z = k if t else (k + 2) % 4
-            v = V(vec.transpose(Zh[0:32, 32 * z:32 * z + 32], T.MM[32 * k:32 * k + 32, mo:mo + 32]))
-        for k in range((0, 1, 4)[t]):
-            v = V(vec.transpose(Zh[0:32, 128 + 32 * k:160 + 32 * k], T.MM[32 * k:32 * k + 32, mo + 32:mo + 64]))
+        if half == 0:
+            for k in range(4):
+                z = k if t else (k + 2) % 4
+                v = V(vec.transpose(Zh[0:32, 32 * z:32 * z + 32], T.MM[32 * k:32 * k + 32, mo:mo + 32]))
+        else:
+            for k in range((0, 1, 4)[t]):
+                v = V(vec.transpose(Zh[0:32, 128 + 32 * k:160 + 32 * k], T.MM[32 * k:32 * k + 32, mo + 32:mo + 64]))
         return v
 
     def b_scan(t, v, aq):
@@ -267,80 +258,90 @@ def rank_program(g, core, T, topo):
                                 bias=T.kb[0:5, t:t + 1], scale=-1.0, accum_out=T.row[0:5, t:t + 1]))
 
     def b_clamp(t, av):
-        X = T.XX[0:5, 32 * t:32 * t + 32]
         W("v", av)
-        v = V(vec.tensor_scalar(X, T.lo[0:5, 32 * t:32 * t + 32], T.row[0:5, t:t + 1], T.hi[0:5, t:t + 1], Op.max, Op.min))
+        v = V(vec.tensor_scalar(T.XX[0:5, 32 * t:32 * t + 32], T.lo[0:5, 32 * t:32 * t + 32], T.row[0:5, t:t + 1],
+                                T.hi[0:5, t:t + 1], Op.max, Op.min))
         W("v", v)
         for k in range(4):
             v = V(vec.transpose(T.BBB[32 * k:32 * k + 32, 32 * t:32 * t + 32], T.XX[0:32, 32 * t:32 * t + 32]))
-        if t < 2:
-            V(vec.tensor_tensor(T.lo[0:5, 32 * t + 32:32 * t + 64], X, T.nhb[0:5, :], Op.subtract))
-            V(vec.tensor_tensor(T.hi[0:5, t + 1:t + 2], T.XX[0:5, 32 * t:32 * t + 1], T.nhb[0:5, 0:1], Op.add))
         return v
 
-    def b_masks(t, cols):
-        MK, MWt = T["MK%d" % t], MW[t]
+    def b_range(t):
+        V(vec.tensor_tensor(T.lo[0:5, 32 * t + 32:32 * t + 64], T.XX[0:5, 32 * t:32 * t + 32], T.nhb[0:5, :], Op.subtract))
+        V(vec.tensor_tensor(T.hi[0:5, t + 1:t + 2], T.XX[0:5, 32 * t:32 * t + 1], T.nhb[0:5, 0:1], Op.add))
+
+    def masks(t, cols):
+        MK = T["MK%d" % t]
         for p, gc, is_left in cols:
             if is_left:
                 v = V(vec.tensor_scalar(MK[:, p:16:4], BO(t - 1, 0, 4), T.gi[:, gc:gc + 1], None, Op.is_le))
             else:
                 v = V(vec.tensor_scalar(MK[:, p:16:4], BO(t - 1, 1, 5), T.gi[:, gc:gc + 1], None, Op.is_gt))
-        W("v", v)
-        for b in range(n - 1):
-            v = V(vec.tensor_tensor(MWt[:, 16 * b:16 * b + 16], MK[:], T.WT1[:, 16 * b:16 * b + 16], Op.mult))
         return v
 
-    V(vec.tensor_scalar(T.lo[0:32, 0:32], T.nhb[0:32, :], -1.0, None, Op.mult))
-    V(vec.tensor_copy(T.hi[0:32, 0:1], T.nhb[0:32, 0:1]))
-    W("a", ("lm0", l_in), vmm, a0, a1)
-    A(act.activation(T.MM[64:128, 33:36], T.L0[64:128, 1:10:4], Act.Copy))
+    lm0 = ("lm0", l_in)
+    W("a", lm0, vmm, a1)
+    A(act.activation(T.MM[64:128, 33:36], T.L0[64:128, 2:11:4], Act.Copy))
     ax = A(act.activation(T.MM[0:64, 33:36], T.L0[0:64, 4:13:4], Act.Copy))
-    vm = b_mult(0, vset, a0, a1)
-    vq, _ = b_red(0, vm)
-    vt = b_tq(0, vq)
-    vt2 = b_tx(0, ax)
-    aq = b_qsum(0, vt)
     halo = ((8, 40, 40), (48, 336, 40))
     hr = relus("a", (0, 2), ph0, 4, T.h1, *halo)
-    hr += relus("v", (1, 3), ph0, 4, T.h1, *halo)
-    ac1 = count(1, 1, 0, pc1)
-    vs = b_scan(0, vt2, aq)
+    vps = b_ps(0, lm0, a1)
+    hr += relus("v", (1,), ph0, 4, T.h1, *halo)
+    vsh = b_share(0, vps)
+    hr += relus("v", (3,), ph0, 4, T.h1, *halo)
     W("v", *hr, *rl)
     vp0 = V(vec.quantize_mx(T.W1[:, 0:128], T.W1s[:, 0:128], T.h1[:, 0:512]))
     vp2 = V(vec.quantize_mx(T.W1[:, 256:384], T.W1s[:, 256:384], T.h1[:, 1024:1536]))
-    av = b_sign(0, vs)
+    vq = b_sub(0, vsh)
+    vt2 = b_tx(0, ax, 0)
+    vt = b_tq(0, vq)
     W("p", vp0)
     pc0 = cost_mm(1, "W1", 0)
     W("p", vp2)
     pc2 = cost_mm(2, "W1", 256)
+    ac1 = count(1, 1, 0, pc1)
     ac0 = count(1, 0, 1, pc0)
     ac2 = count(1, 2, 2, pc2)
+    aq = b_qsum(0, vt)
     W("g", vp2)
     send_ends(1, "nc", "W1", "W1", 120, (40, 512), (256, 384))
     send_ends(1, "ns", "W1", "W1", 120, (40, 512), (256, 384))
     W("g", ac0, ac1, ac2)
     send_costs(1)
-    W("p", *rl, ac0, ac1, ac2)
-    pm = [w_mm(b, b, "W1", 128, 160) for b in range(4)]
+    W("v", gset)
+    vj = V(vec.tensor_scalar(T.pm[:], T.pi[:], 15, None, Op.bitwise_and))
+    V(vec.tensor_scalar(T.lo[0:32, 0:32], T.nhb[0:32, :], -1.0, None, Op.mult))
+    V(vec.tensor_copy(T.hi[0:32, 0:1], T.nhb[0:32, 0:1]))
+    W("v", vj)
+    vj = V(vec.tensor_copy(T.pf[:], T.pm[:]))
+    V(vec.memset(T.MK1[:], 1.0))
+    vs = b_scan(0, vt2, aq)
+    av = b_sign(0, vs)
+    W("v", vj)
+    vj = V(vec.tensor_tensor(T.J[:], T.j0[:], T.pf[:], Op.add))
+    V(vec.memset(T.m2[:, 0:160], 0.0))
     W("v", vj)
     V(vec.tensor_scalar(T.JL[:], T.J[:, 0:8], 2.0, -160.0, Op.mult, Op.add))
     V(vec.tensor_scalar(T.JR[:], T.J[:, 0:8], 2.0, -96.0, Op.mult, Op.add))
     V(vec.tensor_copy(T.Jm[:, 0:8], T.J[:, 0:8]))
     vj = V(vec.tensor_scalar(T.Jm[:, 8:16], T.J[:, 0:8], 288.0, None, Op.add))
+    W("p", *rl, ac0, ac1, ac2)
+    pm = [w_mm(b, b, "W1", 128, 160) for b in range(4)]
     vB = b_clamp(0, av)
     W("v", vB, vj)
     V(vec.tensor_scalar(T.t1[:, 0:8], T.JL[:], BO(0, r, r + 1), 384.0, Op.is_lt, Op.mult))
     vl = V(vec.tensor_scalar(T.t1[:, 8:16], T.JR[:], BO(0, r + 1, r + 2), 216.0, Op.is_ge, Op.mult))
-    V(vec.memset(T.m2[:, 0:160], 0.0))
+    mk1 = masks(1, ((0, 0, True), (2, 0, False)))
     W("v", vl)
     vl = V(vec.tensor_tensor(T.t2[:], T.t1[:], T.Jm[:], Op.add))
-    V(vec.memset(T.m2[:, 1824:2048], 0.0))
+    b_range(0)
     W("v", vl)
     vl = V(vec.tensor_copy(T.la[:], T.t2[:]))
     rm = relus("a", (0, 2), pm, 0, T.m2, (0, 168, 160)) + relus("v", (1, 3), pm, 0, T.m2, (0, 168, 160))
-    mk1 = b_masks(1, ((0, 0, True), (2, 0, False)))
     vpad1 = zeros("W1", *(([384] if left is None else []) + ([512] if right is None else [])))
-    vpad2 = zeros("N2", *pads)
+    V(vec.memset(T.m2[:, 1824:2048], 0.0))
+    V(vec.tensor_scalar(T.J8[:, 0:4], T.J[:, 0:4], 2.0, 240.0, Op.mult, Op.add))
+    vj = V(vec.tensor_scalar(T.J8[:, 4:8], T.J[:, 0:4], 2.0, 624.0, Op.mult, Op.add))
 
     vpk, apk = [], []
     W("v", vl, vp2, vq1, *vpad1, ("nc1", n_in))
@@ -354,19 +355,24 @@ def rank_program(g, core, T, topo):
     pL = [w_mm(4 + b, b, "M1", 0, 128) for b in range(4)]
     W("p", vpk[1], apk[1], *rm)
     pR = [w_mm(b, b, "M1", 128, 128) for b in range(4)]
-    vm = b_mult(1, mk1, ac0, ac1, ac2)
+    vpad2 = zeros("N2", *pads)
+    vm = b_mask(1, mk1, ac0, ac1, ac2)
     rL = relus("a", (0, 2), pL, 4, T.m2, (0, 40, 128)) + relus("v", (1,), pL, 4, T.m2, (0, 40, 128))
-    vq, vxx = b_red(1, vm)
+    vps = b_ps(1, vm)
+    vxx = b_x(1)
     rL += relus("v", (3,), pL, 4, T.m2, (0, 40, 128))
-    vt = b_tq(1, vq)
+    vsh = b_share(1, vps)
     W("v", *rL, *rm)
     vc0 = V(vec.quantize_mx(T.C2[:, 0:256], T.C2s[:, 0:256], T.m2[:, 0:1024]))
-    rR = relus("a", (0,), pR, 0, T.m2, (0, 328, 128))
+    vq = b_sub(1, vsh)
+    rR = relus("v", (1,), pR, 0, T.m2, (0, 328, 128))
+    vt = b_tq(1, vq)
+    rR += relus("a", (0, 2), pR, 0, T.m2, (0, 328, 128)) + relus("v", (3,), pR, 0, T.m2, (0, 328, 128))
     aq = b_qsum(1, vt)
-    rR += relus("a", (2,), pR, 0, T.m2, (0, 328, 128)) + relus("v", (1, 3), pR, 0, T.m2, (0, 328, 128))
-    vt2 = b_tx(1, vxx)
     W("v", *rR)
     vc1 = V(vec.quantize_mx(T.C2[:, 256:512], T.C2s[:, 256:512], T.m2[:, 1024:2048]))
+    b_tx(1, vxx, 0)
+    vt2 = b_tx(1, vxx, 1)
     vs = b_scan(1, vt2, aq)
     W("p", vc0, *rL)
     pc = [cost_mm(4, "C2", 0), cost_mm(5, "C2", 128)]
@@ -379,40 +385,45 @@ def rank_program(g, core, T, topo):
     W("p", *rR)
     pm = [w_mm(b, b, "C2", 40, 416) for b in range(4)]
     ro = relus("a", (0,), pm, 0, T.m3, (0, 0, 416))
-    V(vec.tensor_scalar(T.J8[:, 0:4], T.J[:, 0:4], 2.0, 240.0, Op.mult, Op.add))
-    vj = V(vec.tensor_scalar(T.J8[:, 4:8], T.J[:, 0:4], 2.0, 624.0, Op.mult, Op.add))
     V(vec.tensor_scalar(T.J2[:], T.J[:], 2.0, None, Op.mult))
     V(vec.tensor_scalar(T.J2m[:], T.J[:], 2.0, -512.0, Op.mult, Op.add))
-    vz = V(vec.memset(T.hh2[:, 320:512], 0.0))
+    vhz = V(vec.memset(T.hh2[:, 320:512], 0.0))
     vB = b_clamp(1, av)
     W("v", vB, vj)
     V(vec.tensor_scalar(T.lb[:, 0:4], T.J8[:, 0:4], BO(1, r, r + 1), 0.5, Op.add, Op.mult))
     vl = V(vec.tensor_scalar(T.lb[:, 4:8], T.J8[:, 4:8], BO(1, r + 1, r + 2), 0.5, Op.add, Op.mult))
+    mk2 = masks(2, ((0, 1, True), (1, 2, True), (2, 1, False), (3, 2, False)))
     W("v", vl)
     vh = V(vec.tensor_copy(T.H2[:].bitcast(dt.uint32), T.C2[:, 0:512].bitcast(dt.uint32).indirect(T.lb[:, 0:8])))
+    W("v", mk2)
+    for b in range(n - 1):
+        vw = V(vec.tensor_tensor(T.MW[:, 16 * b:16 * b + 16], T.MK2[:], T.WT[:, 16 * b:16 * b + 16], Op.mult))
     W("a", vl, vc1)
     ah = A(act.activation(T.H2s[:], T.C2s[:, 0:512].indirect(T.lb[:, 0:8]), Act.Copy))
     W("g", vh)
     send_ends(2, "nc", "H2", "N2", 48, (0, 176), (80, 128))
     W("g", ah)
     send_ends(2, "ns", "H2", "N2", 48, (0, 176), (80, 128))
-    mk2 = b_masks(2, ((0, 1, True), (1, 2, True), (2, 1, False), (3, 2, False)))
-    V(vec.tensor_scalar(T.kk[:, 0:1], BO(1, r, r + 1), -0.5, 376.0, Op.mult, Op.add))
-    vk = V(vec.tensor_scalar(T.kk[:, 1:2], BO(1, r + 1, r + 2), -0.5, 120.0, Op.mult, Op.add))
+    ro += relus("a", (1, 2, 3), pm, 0, T.m3, (0, 0, 416))
 
-    def bd_row(t):
-        W("v", V(vec.tensor_scalar(T.Bh[:, 5 * t:5 * t + 5], BO(t, 0, 5), 0.5, None, Op.mult)))
-        return V(vec.tensor_tensor(T.Ball[:, 5 * t:5 * t + 5], T.Bh[:, 5 * t:5 * t + 5], T.B0[:], Op.add))
-
-    ro += relus("a", (2,), pm, 0, T.m3, (0, 0, 416)) + relus("v", (1,), pm, 0, T.m3, (0, 0, 416))
-    vm = b_mult(2, mk2, *ac)
-    vq, vxx = b_red(2, vm)
+    W("v", ("lm2", l_in), vw, *ac)
+    for b in range(n - 1):
+        vw = V(vec.tensor_tensor(T.LW[:, 16 * b:16 * b + 16], T.L2[:], T.MW[:, 16 * b:16 * b + 16], Op.mult))
+    vm = b_mask(2)
+    W("v", vw)
+    for b in range(n - 1):
+        vq = V(vec.tensor_reduce(T.MM[:, 193 + b:194 + b], T.LW[:, 16 * b:16 * b + 16], AxisListType.X, Op.add))
+    W("v", vm)
+    vxx = b_x(2)
     vt = b_tq(2, vq)
-    vt2 = b_tx(2, vxx)
+    b_tx(2, vxx, 0)
+    vt2 = b_tx(2, vxx, 1)
+    b_range(1)
     aq = b_qsum(2, vt)
-    ro += relus("a", (3,), pm, 0, T.m3, (0, 0, 416))
     vs = b_scan(2, vt2, aq)
     av = b_sign(2, vs)
+    V(vec.tensor_scalar(T.kk[:, 0:1], BO(1, r, r + 1), -0.5, 376.0, Op.mult, Op.add))
+    vk = V(vec.tensor_scalar(T.kk[:, 1:2], BO(1, r + 1, r + 2), -0.5, 120.0, Op.mult, Op.add))
     W("p", *vpad2, *ac, ("nc2", n_in), ("ns2", n_in))
     ph = [w_mm(4 + b, b, "N2", 128, 128) for b in range(4)]
     W("v", *ro)
@@ -420,12 +431,15 @@ def rank_program(g, core, T, topo):
     h2 = relus("a", (0, 2), ph, 4, T.hh2, (8, 0, 80))
     vB = b_clamp(2, av)
     h2 += relus("v", (1, 3), ph, 4, T.hh2, (8, 0, 80))
+    W("a", vB)
+    for t in range(3):
+        ab = A(act.activation(T.Bh[:, 5 * t:5 * t + 5], BO(t, 0, 5), Act.Copy, scale=0.5))
     W("v", vB, vk)
     U2, V2, U = T.terms[:, 0:31], T.terms[:, 31:62], T.terms[:, 62:93]
     V(vec.tensor_scalar(U2, T.J2[:], BO(2, r, r + 1), None, Op.add))
     V(vec.tensor_scalar(V2, T.J2m[:], BO(2, r, r + 1), None, Op.add))
     vu = V(vec.tensor_scalar(U, T.J2[:], BO(2, r, r + 1), 0.5, Op.add, Op.mult))
-    W("v", vz, *h2)
+    W("v", vhz, *h2)
     vch = V(vec.quantize_mx(T.C3[:, 416:544], T.C3s[:, 416:544], T.hh2[:]))
     W("v", vu)
     V(vec.tensor_scalar(T.terms[:, 93:124], U2, BO(1, r, r + 1), T.kk[:, 0:1], Op.is_lt, Op.mult))
@@ -437,44 +451,39 @@ def rank_program(g, core, T, topo):
     vu = V(vec.tensor_tensor(T.sum1[:, 0:31], T.sum3[:, 0:31], T.sum3[:, 31:62], Op.add))
     W("v", vu)
     vl = V(vec.tensor_scalar(T.lf[:, 0:31], T.sum1[:, 0:31], 80.0, 500.0, Op.add, Op.min))
+    W("v", ab)
+    vN = V(vec.tensor_tensor(T.Ball[:, 0:15], T.Bh[:, 0:15], T.B0[:], Op.add))
+    W("p", vc3, *ro)
+    py = P(ten.matmul_mx(bank(0, 0, 416), T.qa[:], T.qas[:], T.C3[:, 0:416], T.C3s[:, 0:416], True, True))
+    W("p", vch)
+    pz = P(ten.matmul_mx(bank(1, 0, 128), T.qa[:], T.qas[:], T.C3[:, 416:544], T.C3s[:, 416:544], True, True))
+    W("a", py)
+    A(act.activation(T.YC[:, 0:416], bank(0, 0, 416), Act.Copy))
+    W("a", pz)
+    yc = A(act.activation(T.YC[:, 416:544], bank(1, 0, 128), Act.Copy))
+
     W("v", vl, vch, vc3)
     W("a", vl, vch, vc3)
-    halves = (("FA", 0, 256), ("FB", 256, 496))
-    vf, af, py = [], [], []
-    for F, a, b in halves:
+    halves = ((0, 256), (256, 496))
+    vf, af = [], []
+    for a, b in halves:
         l = T.lf[:, a // 16:b // 16]
-        vf.append(V(vec.tensor_copy(T[F][:].bitcast(dt.uint32), T.C3[:, 0:544].bitcast(dt.uint32).indirect(l))))
-        af.append(A(act.activation(T[F + "s"][:], T.C3s[:, 0:544].indirect(l), Act.Copy)))
-    W("p", *ro)
-    for k, (F, a, b) in enumerate(halves):
-        W("p", vf[k], af[k])
-        py.append(P(ten.matmul_mx(bank(k, 0, b - a), T.qa[:], T.qas[:], T[F][:], T[F + "s"][:], True, True)))
-    bd_row(0)
-    bd_row(1)
-    vN = bd_row(2)
-    W("v", py[0])
-    vy = V(vec.tensor_copy(T.yt[:, 0:256], bank(0, 0, 256)))
-    W("a", py[1])
-    ay = A(act.activation(T.yt[:, 256:496], bank(1, 0, 240), Act.Copy))
-
-    def out_codes(k):
-        F, a, b = halves[k]
-        W("s", vf[k])
-        inc("dout", g.sync.dma_start(T.oc[:, 4 * a:4 * b], T[F][:].bitcast(dt.uint8)), 16)
-
-    def out_scales(q, k):
-        F, a, b = halves[k]
-        W(q, af[k])
-        for i in range(4):
-            inc("dout", queue[q].dma_start(T.osc[4 * i:4 * i + 4, a:b], T[F + "s"][32 * i:32 * i + 4, :]), 16)
-    out_codes(0)
-    out_scales("s", 0)
-    out_codes(1)
+        vf.append(V(vec.tensor_copy(T.F[:, a:b].bitcast(dt.uint32), T.C3[:, 0:544].bitcast(dt.uint32).indirect(l))))
+        af.append(A(act.activation(T.Fs[:, a:b], T.C3s[:, 0:544].indirect(l), Act.Copy)))
+    W("v", yc)
+    W("a", yc)
+    vy = V(vec.tensor_copy(T.yt[:, 0:256], T.YC[:, 0:544].indirect(T.lf[:, 0:16])))
+    ay = A(act.activation(T.yt[:, 256:496], T.YC[:, 0:544].indirect(T.lf[:, 16:31]), Act.Copy))
     W("s", vN)
     inc("dout", g.sync.dma_start(T.bd[:], T.Ball[0:1, 0:15]), 16)
+    for k, (a, b) in enumerate(halves):
+        W("s", vf[k])
+        inc("dout", g.sync.dma_start(T.oc[:, 4 * a:4 * b], T.F[:, a:b].bitcast(dt.uint8)), 16)
+    W("s", af[1])
+    for i in range(4):
+        inc("dout", g.sync.dma_start(T.osc[4 * i:4 * i + 4, :], T.Fs[32 * i:32 * i + 4, :]), 16)
     W("s", vy)
     inc("dout", g.sync.dma_start(T.y[:, 0:256], T.yt[:, 0:256]), 16)
     W("a", ay)
     inc("dout", act.dma_start(T.y[:, 256:496], T.yt[:, 256:496]), 16)
-    out_scales("a", 1)
     W("g", *[(s, c) for s, c in cnt.items()])

import numpy as np
from concourse.bass import DstId, RemoteDMATransfer
from concourse.mybir import dt, AluOpType as Op, AxisListType, ActivationFunctionType as Act

F32, BF, I32, U16, F8, U8 = "float32", "bfloat16", "int32", "uint16", "float8_e4m3fn_x4", "uint8"
SCRATCH = {"ps": ("psum", [128, 4096], F32)}
for _names, _d in (("xt:1024 at:512 wt:2048 h1:1536 m2:2048 m3:1664 hh2:512 zt:512 junk:1408", BF),
                   ("eps:4 kb:4 c130:256 nh:32 nha:32 nhb:32 MM:288 XX:96 lo:96 hi:4 BBB:96 row:16 rjunk:1536 B0:15 Bh:16 Ball:16 "
                    "pf:31 j0:31 J:31 J2:31 J2m:31 JL:8 JR:8 Jm:16 J8:8 gi:4 wq:4 z16:16 WT:48 MW:48 LW:48 MK1:16 MK2:16 "
                    "LM:48 PS:48 TW:16 t1:16 t2:16 kk:4 terms:192 sum3:64 sum1:32 yt:512 YC:544 L0:16 L1:16 L2:16 "
                    "Zq0:128 Zq1:128 Zq2:128 Zh0:128 Zh1:160 Zh2:256 Ih0:132 Ih1:164 Ih2:244", F32),
                   ("pi:31 pm:31", I32), ("la:16 lb:8 lf:32", U16)):
    for _s in _names.split():
        SCRATCH[_s.split(":")[0]] = ("sbuf", [128, int(_s.split(":")[1])], _d)
for _n, _w in (("qa", 128), ("qw", 512), ("C0", 256), ("W1", 640), ("M1", 256), ("C2", 512), ("C3", 544), ("H2", 128),
               ("N0", 352), ("N2", 352), ("F", 496)):
    SCRATCH[_n] = ("sbuf", [128, _w], F8)
    SCRATCH[_n + "s"] = ("sbuf", [128, _w], U8)
SEMAPHORES = ["sv", "sa", "sp", "gc", "dx0", "dx1", "da", "dw", "dout", "ls"] + \
    ["%s%d" % (n, t) for n in ("nc", "ns", "lm") for t in range(3)]
HALF = (64, 80, 120)
MOVE = (40, 80, 120)


def rank_program(g, core, T, topo):
    r = T.rank_of(core)
    if r is None:
        return
    n = len(T.cores)
    left, right = (r - 1 if r else None), (r + 1 if r < n - 1 else None)
    vec, act, ten = g.vector, g.scalar, g.tensor
    queue = {"v": vec, "a": act, "p": ten, "g": g, "s": g.sync}
    cnt, seen = {}, {q: {} for q in queue}

    def W(q, *toks):
        need = {}
        for s, c in toks:
            need[s] = max(need.get(s, 0), c)
        for s, c in need.items():
            if seen[q].get(s, 0) < c:
                queue[q].wait_ge(T.sem[s], c)
                seen[q][s] = c

    def inc(sem, ins, k=1):
        ins.then_inc(T.sem[sem], k)
        cnt[sem] = cnt.get(sem, 0) + k
        return (sem, cnt[sem])

    V = lambda ins: inc("sv", ins)
    A = lambda ins: inc("sa", ins)
    P = lambda ins: inc("sp", ins)
    G = lambda ins: inc("gc", ins)
    bank = lambda k, a, b: T.ps[:, 512 * k + a:512 * k + b]

    def nbs(q):
        return [p for p in (q - 1, q + 1) if 0 <= p < n]

    def engs(q, p):
        e = topo.engines(T.cores[q], T.cores[p])
        k = len(e) // len(nbs(q))
        i = nbs(q).index(p)
        return e[k * i:k * i + k]

    def did(p):
        rid, pnc, _ = topo.addr(T.cores[p])
        return DstId(rid=rid, pnc=pnc)

    def send_ends(t, name, src, dst, w, to_left, to_right):
        tr = []
        for p in nbs(r):
            a, c = to_left if p < r else to_right
            if name == "nc":
                s, d = T[src][:, a:a + w].bitcast(dt.uint8), T[dst][:, c:c + w].bitcast(dt.uint8)
            else:
                s, d = T[src + "s"][:, a:a + w], T[dst + "s"][:, c:c + w]
            e = engs(r, p)
            tr.append(RemoteDMATransfer(dst_ids=[did(p)], dma_engine_mask=sum(1 << i for i in e),
                                        remote_sem=T.sem["%s%d" % (name, t)], src=s, dst=d))
            cnt["ls"] = cnt.get("ls", 0) + len(e)
        g.remote_dma_fused(tr, local_sem=T.sem.ls)

    others = [p for p in range(n) if p != r]

    def send_costs(t):
        s = T["L%d" % t][:, 4 * r:4 * r + 4]
        e = topo.engines(T.cores[r], T.cores[others[0]])
        g.remote_dma_fused([RemoteDMATransfer(dst_ids=[did(p) for p in others], dma_engine_mask=sum(1 << i for i in e),
                                              remote_sem=T.sem["lm%d" % t], srcs=[s], dsts=[s for p in others])],
                           local_sem=T.sem.ls)
        cnt["ls"] = cnt.get("ls", 0) + len(e)

    n_in = sum(len(engs(p, r)) for p in nbs(r))
    l_in = sum(len(topo.engines(T.cores[p], T.cores[r])) for p in others)

    kx0 = inc("dx0", g.sync.dma_start(T.xt[:, 0:512], T.x[:, 0:512]), 16)
    kx1 = inc("dx1", act.dma_start(T.xt[:, 512:1024], T.x[:, 512:1024]), 16)
    ka = inc("da", g.sync.dma_start(T.at[:], T.a[:]), 16)
    inc("dw", act.dma_start(T.wt[:, 1024:2048], T.w[:, 1024:2048]), 16)
    kw = inc("dw", g.sync.dma_start(T.wt[:, 0:1024], T.w[:, 0:1024]), 16)

    def zeros(name, *cols):
        return [V(vec.quantize_mx(T[name][:, a:a + 128], T[name + "s"][:, a:a + 128], T.zt[:])) for a in cols]
    pads = ([48] if left is None else []) + [224 if right is not None else 176]
    vnh = V(vec.memset(T.nh[0:32, :], 80.0))
    vz = V(vec.memset(T.zt[:], 0.0))
    for t in range(3):
        V(vec.memset(T["L%d" % t][:, 4 * r:4 * r + 4], 0.0))
    veps = V(vec.memset(T.eps[:, 0:1], -(2.0 ** -120)))
    for b in range(1, n):
        k, c = 16 * (b - 1), 4 * (b - 1) + 2
        V(vec.memset(T.WT[:, k:k + c], 1 - b / 4.0))
        V(vec.memset(T.WT[:, k + c:k + 16], -b / 4.0))
    W("v", vz)
    vpad0 = zeros("N0", *pads)
    G(g.iota(T.pi[:], [[0, 31]], 0, 1))
    G(g.iota(T.j0[:], [[16, 31]], 0, 0, allow_small_or_imprecise_dtypes=True))
    G(g.iota(T.B0[:], [[0, 3], [256, 5]], 0, 0, allow_small_or_imprecise_dtypes=True))
    for k, b0 in enumerate((-160, -240, 16)):
        G(g.iota(T.gi[:, k:k + 1], [[0, 1]], b0, 2, allow_small_or_imprecise_dtypes=True))
    W("g", vnh)
    gk = G(g.affine_select(T.nha[0:32, :], T.nh[0:32, :], [[0, 32]], Op.is_ge, 0.0, -1, 1))
    W("g", gk)
    gset = G(g.affine_select(T.nhb[0:32, :], T.nha[0:32, :], [[0, 32]], Op.is_ge, 0.0, n - 1, -1))

    W("v", kx0)
    V(vec.quantize_mx(T.C0[:, 0:128], T.C0s[:, 0:128], T.xt[:, 0:512]))
    W("v", kx1)
    vx = V(vec.quantize_mx(T.C0[:, 128:256], T.C0s[:, 128:256], T.xt[:, 512:1024]))
    W("v", ka)
    va = V(vec.quantize_mx(T.qa[:], T.qas[:], T.at[:]))
    W("g", vx)
    send_ends(0, "nc", "C0", "N0", 48, (0, 176), (208, 128))
    send_ends(0, "ns", "C0", "N0", 48, (0, 176), (208, 128))

    def cost_mm(k, name, a):
        return P(ten.matmul_mx(bank(k, 0, 128), T[name][:, a:a + 128], T[name + "s"][:, a:a + 128], T.qa[:], T.qas[:], True, True))

    junk = []

    def count(t, piece, k, tok, a=0, b=128):
        W("a", tok)
        j = 128 * len(junk)
        junk.append(j)
        c = 4 * r + piece
        return A(act.activation(T.junk[a:b, j:j + 128], T.ps[a:b, 512 * k:512 * k + 128], Act.Sign, bias=T.eps[a:b, 0:1],
                                accum_out=T["L%d" % t][a:b, c:c + 1]))

    W("p", va)
    p0, p1 = cost_mm(4, "C0", 0), cost_mm(5, "C0", 128)
    W("a", veps)
    count(0, 0, 4, p0)
    count(0, 1, 5, p1, 0, 64)
    a1 = count(0, 2, 5, p1, 64, 128)
    W("g", a1)
    send_costs(0)

    V(vec.memset(T.h1[:, 0:160], 0.0))
    V(vec.memset(T.h1[:, 1504:1536], 0.0))
    vmm = V(vec.memset(T.MM[:], 0.0))
    V(vec.memset(T.XX[0:32, :], 0.0))
    W("v", kw)
    vw = V(vec.quantize_mx(T.qw[:], T.qws[:], T.wt[:]))

    def w_mm(k, b, name, a, m):
        return P(ten.matmul_mx(bank(k, 0, m), T.qw[:, 128 * b:128 * b + 128], T.qws[:, 128 * b:128 * b + 128],
                               T[name][:, a:a + m], T[name + "s"][:, a:a + m], True, True))

    def relu(q, out, src):
        if q == "a":
            return A(act.activation(out, src, Act.Relu, scale=0.0625))
        return V(vec.tensor_scalar(out, src, 0.0, 0.0625, Op.max, Op.mult))

    def relus(q, bs, pm, k0, h, *runs):
        out = []
        for b in bs:
            W(q, pm[b])
            for a, c, m in runs:
                out.append(relu(q, h[:, 4 * c + b:4 * (c + m):4], bank(k0 + b, a, a + m)))
        return out

    W("p", vx, vw)
    pm = [w_mm(b, b, "C0", 0, 256) for b in range(4)]
    V(vec.memset(T.z16[:], 0.0))
    for b in range(1, n):
        V(vec.memset(T.wq[:, b - 1:b], b / 4.0))
    V(vec.memset(T.c130[0:32, :], 130.0))
    rl = relus("a", (0, 2), pm, 0, T.h1, (0, 80, 256)) + relus("v", (1, 3), pm, 0, T.h1, (0, 80, 256))
    W("v", *rl)
    vq1 = V(vec.quantize_mx(T.W1[:, 128:256], T.W1s[:, 128:256], T.h1[:, 512:1024]))
    for t in range(3):
        V(vec.memset(T.kb[0:32, t:t + 1], 130.0 * HALF[t] - 0.125))
    W("p", *vpad0, a1, ("nc0", n_in), ("ns0", n_in))
    ph0 = [w_mm(4 + b, b, "N0", 128, 128) for b in range(4)]
    W("p", vq1, *rl)
    pc1 = cost_mm(0, "W1", 128)

    BO = lambda t, a, b: T.BBB[:, 32 * t + a:32 * t + b]

    def b_mask(t, *toks):
        W("v", ("lm%d" % t, l_in), *toks)
        return V(vec.tensor_tensor(T.LM[:, 16 * t:16 * t + 16], T["L%d" % t][:], T["MK%d" % t][:], Op.mult))

    def b_ps(t, *toks):
        W("v", *toks)
        src = T.LM[:, 16 * t:16 * t + 16] if t else T.L0[:]
        return V(vec.tensor_tensor_scan(T.PS[:, 16 * t:16 * t + 16], src, T.z16[:], 0.0, Op.add, Op.add))

    def b_x(t):
        m, mo = 16 * t, 96 * t
        v = V(vec.tensor_tensor(T.MM[:, mo + 33:mo + 36], T.LM[:, m + 2:m + 11:4], T.LM[:, m + 4:m + 13:4], Op.add))
        if t == 1:
            return V(vec.tensor_copy(T.MM[0:32, mo + 65:mo + 68], T.L1[0:32, 5:14:4]))
        return V(vec.tensor_tensor(T.MM[:, mo + 65:mo + 68], T.LM[:, m + 3:m + 12:4], T.LM[:, m + 5:m + 14:4], Op.add))

    def b_share(t, v):
        W("v", v)
        return V(vec.tensor_scalar(T.TW[:, 4 * t:4 * t + 3], T.wq[:, 0:3], T.PS[:, 16 * t + 15:16 * t + 16], None, Op.mult))

    def b_sub(t, v):
        W("v", v)
        return V(vec.tensor_tensor(T.MM[:, 96 * t + 1:96 * t + 4], T.PS[:, 16 * t + 1:16 * t + 10:4], T.TW[:, 4 * t:4 * t + 3],
                                   Op.subtract))

    def b_tq(t, vq):
        mo = 96 * t
        W("v", vq)
        for k in range(4):
            v = V(vec.transpose(T["Zq%d" % t][0:32, 32 * k:32 * k + 32], T.MM[32 * k:32 * k + 32, mo:mo + 32]))
        return v

    def b_qsum(t, v):
        W("a", v)
        return A(act.activation(T.rjunk[0:5, 512 * t:512 * t + 128], T["Zq%d" % t][0:5, :], Act.Copy,
                                accum_out=T["Ih%d" % t][0:5, 0:1]))

    def b_tx(t, vxx, half):
        mo, Zh = 96 * t + 32, T["Zh%d" % t]
        W("v", vxx)
        if half == 0:
            for k in range(4):
                z = k if t else (k + 2) % 4
                v = V(vec.transpose(Zh[0:32, 32 * z:32 * z + 32], T.MM[32 * k:32 * k + 32, mo:mo + 32]))
        else:
            for k in range((0, 1, 4)[t]):
                v = V(vec.transpose(Zh[0:32, 128 + 32 * k:160 + 32 * k], T.MM[32 * k:32 * k + 32, mo + 32:mo + 64]))
        return v

    def b_scan(t, v, aq):
        h = 2 * HALF[t]
        Ih = T["Ih%d" % t]
        W("v", v, aq)
        return V(vec.tensor_tensor_scan(Ih[0:5, 1:1 + h], T["Zh%d" % t][0:5, 0:h], T.c130[0:5, 0:h], Ih[0:5, 0:1], Op.add, Op.add))

    def b_sign(t, v):
        a, w = HALF[t] - MOVE[t], 2 * MOVE[t]
        W("a", v)
        return A(act.activation(T.rjunk[0:5, 512 * t + 128:512 * t + 128 + w], T["Ih%d" % t][0:5, a:a + w], Act.Sign,
                                bias=T.kb[0:5, t:t + 1], scale=-1.0, accum_out=T.row[0:5, t:t + 1]))

    def b_clamp(t, av):
        W("v", av)
        v = V(vec.tensor_scalar(T.XX[0:5, 32 * t:32 * t + 32], T.lo[0:5, 32 * t:32 * t + 32], T.row[0:5, t:t + 1],
                                T.hi[0:5, t:t + 1], Op.max, Op.min))
        W("v", v)
        for k in range(4):
            v = V(vec.transpose(T.BBB[32 * k:32 * k + 32, 32 * t:32 * t + 32], T.XX[0:32, 32 * t:32 * t + 32]))
        return v

    def b_range(t):
        V(vec.tensor_tensor(T.lo[0:5, 32 * t + 32:32 * t + 64], T.XX[0:5, 32 * t:32 * t + 32], T.nhb[0:5, :], Op.subtract))
        V(vec.tensor_tensor(T.hi[0:5, t + 1:t + 2], T.XX[0:5, 32 * t:32 * t + 1], T.nhb[0:5, 0:1], Op.add))

    def masks(t, cols):
        MK = T["MK%d" % t]
        for p, gc, is_left in cols:
            if is_left:
                v = V(vec.tensor_scalar(MK[:, p:16:4], BO(t - 1, 0, 4), T.gi[:, gc:gc + 1], None, Op.is_le))
            else:
                v = V(vec.tensor_scalar(MK[:, p:16:4], BO(t - 1, 1, 5), T.gi[:, gc:gc + 1], None, Op.is_gt))
        return v

    lm0 = ("lm0", l_in)
    W("a", lm0, vmm, a1)
    A(act.activation(T.MM[64:128, 33:36], T.L0[64:128, 2:11:4], Act.Copy))
    ax = A(act.activation(T.MM[0:64, 33:36], T.L0[0:64, 4:13:4], Act.Copy))
    halo = ((8, 40, 40), (48, 336, 40))
    hr = relus("a", (0, 2), ph0, 4, T.h1, *halo)
    vps = b_ps(0, lm0, a1)
    hr += relus("v", (1,), ph0, 4, T.h1, *halo)
    vsh = b_share(0, vps)
    hr += relus("v", (3,), ph0, 4, T.h1, *halo)
    W("v", *hr, *rl)
    vp0 = V(vec.quantize_mx(T.W1[:, 0:128], T.W1s[:, 0:128], T.h1[:, 0:512]))
    vp2 = V(vec.quantize_mx(T.W1[:, 256:384], T.W1s[:, 256:384], T.h1[:, 1024:1536]))
    vq = b_sub(0, vsh)
    vt2 = b_tx(0, ax, 0)
    vt = b_tq(0, vq)
    W("p", vp0)
    pc0 = cost_mm(1, "W1", 0)
    W("p", vp2)
    pc2 = cost_mm(2, "W1", 256)
    ac1 = count(1, 1, 0, pc1)
    ac0 = count(1, 0, 1, pc0)
    ac2 = count(1, 2, 2, pc2)
    aq = b_qsum(0, vt)
    W("g", vp2)
    send_ends(1, "nc", "W1", "W1", 120, (40, 512), (256, 384))
    send_ends(1, "ns", "W1", "W1", 120, (40, 512), (256, 384))
    W("g", ac0, ac1, ac2)
    send_costs(1)
    W("v", gset)
    vj = V(vec.tensor_scalar(T.pm[:], T.pi[:], 15, None, Op.bitwise_and))
    V(vec.tensor_scalar(T.lo[0:32, 0:32], T.nhb[0:32, :], -1.0, None, Op.mult))
    V(vec.tensor_copy(T.hi[0:32, 0:1], T.nhb[0:32, 0:1]))
    W("v", vj)
    vj = V(vec.tensor_copy(T.pf[:], T.pm[:]))
    V(vec.memset(T.MK1[:], 1.0))
    vs = b_scan(0, vt2, aq)
    av = b_sign(0, vs)
    W("v", vj)
    vj = V(vec.tensor_tensor(T.J[:], T.j0[:], T.pf[:], Op.add))
    V(vec.memset(T.m2[:, 0:160], 0.0))
    W("v", vj)
    V(vec.tensor_scalar(T.JL[:], T.J[:, 0:8], 2.0, -160.0, Op.mult, Op.add))
    V(vec.tensor_scalar(T.JR[:], T.J[:, 0:8], 2.0, -96.0, Op.mult, Op.add))
    V(vec.tensor_copy(T.Jm[:, 0:8], T.J[:, 0:8]))
    vj = V(vec.tensor_scalar(T.Jm[:, 8:16], T.J[:, 0:8], 288.0, None, Op.add))
    W("p", *rl, ac0, ac1, ac2)
    pm = [w_mm(b, b, "W1", 128, 160) for b in range(4)]
    vB = b_clamp(0, av)
    W("v", vB, vj)
    V(vec.tensor_scalar(T.t1[:, 0:8], T.JL[:], BO(0, r, r + 1), 384.0, Op.is_lt, Op.mult))
    vl = V(vec.tensor_scalar(T.t1[:, 8:16], T.JR[:], BO(0, r + 1, r + 2), 216.0, Op.is_ge, Op.mult))
    mk1 = masks(1, ((0, 0, True), (2, 0, False)))
    W("v", vl)
    vl = V(vec.tensor_tensor(T.t2[:], T.t1[:], T.Jm[:], Op.add))
    b_range(0)
    W("v", vl)
    vl = V(vec.tensor_copy(T.la[:], T.t2[:]))
    rm = relus("a", (0, 2), pm, 0, T.m2, (0, 168, 160)) + relus("v", (1, 3), pm, 0, T.m2, (0, 168, 160))
    vpad1 = zeros("W1", *(([384] if left is None else []) + ([512] if right is None else [])))
    V(vec.memset(T.m2[:, 1824:2048], 0.0))
    V(vec.tensor_scalar(T.J8[:, 0:4], T.J[:, 0:4], 2.0, 240.0, Op.mult, Op.add))
    vj = V(vec.tensor_scalar(T.J8[:, 4:8], T.J[:, 0:4], 2.0, 624.0, Op.mult, Op.add))

    vpk, apk = [], []
    W("v", vl, vp2, vq1, *vpad1, ("nc1", n_in))
    W("a", vl, vp2, vq1, *vpad1, ("ns1", n_in))
    for k in (0, 1):
        s = slice(128 * k, 128 * k + 128)
        l = T.la[:, 8 * k:8 * k + 8]
        vpk.append(V(vec.tensor_copy(T.M1[:, s].bitcast(dt.uint32), T.W1[:, 0:640].bitcast(dt.uint32).indirect(l))))
        apk.append(A(act.activation(T.M1s[:, s], T.W1s[:, 0:640].indirect(l), Act.Copy)))
    W("p", vpk[0], apk[0], *hr)
    pL = [w_mm(4 + b, b, "M1", 0, 128) for b in range(4)]
    W("p", vpk[1], apk[1], *rm)
    pR = [w_mm(b, b, "M1", 128, 128) for b in range(4)]
    vpad2 = zeros("N2", *pads)
    vm = b_mask(1, mk1, ac0, ac1, ac2)
    rL = relus("a", (0, 2), pL, 4, T.m2, (0, 40, 128)) + relus("v", (1,), pL, 4, T.m2, (0, 40, 128))
    vps = b_ps(1, vm)
    vxx = b_x(1)
    rL += relus("v", (3,), pL, 4, T.m2, (0, 40, 128))
    vsh = b_share(1, vps)
    W("v", *rL, *rm)
    vc0 = V(vec.quantize_mx(T.C2[:, 0:256], T.C2s[:, 0:256], T.m2[:, 0:1024]))
    vq = b_sub(1, vsh)
    rR = relus("v", (1,), pR, 0, T.m2, (0, 328, 128))
    vt = b_tq(1, vq)
    rR += relus("a", (0, 2), pR, 0, T.m2, (0, 328, 128)) + relus("v", (3,), pR, 0, T.m2, (0, 328, 128))
    aq = b_qsum(1, vt)
    W("v", *rR)
    vc1 = V(vec.quantize_mx(T.C2[:, 256:512], T.C2s[:, 256:512], T.m2[:, 1024:2048]))
    b_tx(1, vxx, 0)
    vt2 = b_tx(1, vxx, 1)
    vs = b_scan(1, vt2, aq)
    W("p", vc0, *rL)
    pc = [cost_mm(4, "C2", 0), cost_mm(5, "C2", 128)]
    W("p", vc1)
    pc += [cost_mm(6, "C2", 256), cost_mm(7, "C2", 384)]
    ac = [count(2, k, 4 + k, pc[k]) for k in range(4)]
    av = b_sign(1, vs)
    W("g", *ac)
    send_costs(2)
    W("p", *rR)
    pm = [w_mm(b, b, "C2", 40, 416) for b in range(4)]
    ro = relus("a", (0,), pm, 0, T.m3, (0, 0, 416))
    V(vec.tensor_scalar(T.J2[:], T.J[:], 2.0, None, Op.mult))
    V(vec.tensor_scalar(T.J2m[:], T.J[:], 2.0, -512.0, Op.mult, Op.add))
    vhz = V(vec.memset(T.hh2[:, 320:512], 0.0))
    vB = b_clamp(1, av)
    W("v", vB, vj)
    V(vec.tensor_scalar(T.lb[:, 0:4], T.J8[:, 0:4], BO(1, r, r + 1), 0.5, Op.add, Op.mult))
    vl = V(vec.tensor_scalar(T.lb[:, 4:8], T.J8[:, 4:8], BO(1, r + 1, r + 2), 0.5, Op.add, Op.mult))
    mk2 = masks(2, ((0, 1, True), (1, 2, True), (2, 1, False), (3, 2, False)))
    W("v", vl)
    vh = V(vec.tensor_copy(T.H2[:].bitcast(dt.uint32), T.C2[:, 0:512].bitcast(dt.uint32).indirect(T.lb[:, 0:8])))
    W("v", mk2)
    for b in range(n - 1):
        vw = V(vec.tensor_tensor(T.MW[:, 16 * b:16 * b + 16], T.MK2[:], T.WT[:, 16 * b:16 * b + 16], Op.mult))
    W("a", vl, vc1)
    ah = A(act.activation(T.H2s[:], T.C2s[:, 0:512].indirect(T.lb[:, 0:8]), Act.Copy))
    W("g", vh)
    send_ends(2, "nc", "H2", "N2", 48, (0, 176), (80, 128))
    W("g", ah)
    send_ends(2, "ns", "H2", "N2", 48, (0, 176), (80, 128))
    ro += relus("a", (1, 2, 3), pm, 0, T.m3, (0, 0, 416))

    W("v", ("lm2", l_in), vw, *ac)
    for b in range(n - 1):
        vw = V(vec.tensor_tensor(T.LW[:, 16 * b:16 * b + 16], T.L2[:], T.MW[:, 16 * b:16 * b + 16], Op.mult))
    vm = b_mask(2)
    W("v", vw)
    for b in range(n - 1):
        vq = V(vec.tensor_reduce(T.MM[:, 193 + b:194 + b], T.LW[:, 16 * b:16 * b + 16], AxisListType.X, Op.add))
    W("v", vm)
    vxx = b_x(2)
    vt = b_tq(2, vq)
    b_tx(2, vxx, 0)
    vt2 = b_tx(2, vxx, 1)
    b_range(1)
    aq = b_qsum(2, vt)
    vs = b_scan(2, vt2, aq)
    av = b_sign(2, vs)
    V(vec.tensor_scalar(T.kk[:, 0:1], BO(1, r, r + 1), -0.5, 376.0, Op.mult, Op.add))
    vk = V(vec.tensor_scalar(T.kk[:, 1:2], BO(1, r + 1, r + 2), -0.5, 120.0, Op.mult, Op.add))
    W("p", *vpad2, *ac, ("nc2", n_in), ("ns2", n_in))
    ph = [w_mm(4 + b, b, "N2", 128, 128) for b in range(4)]
    W("v", *ro)
    vc3 = V(vec.quantize_mx(T.C3[:, 0:416], T.C3s[:, 0:416], T.m3[:]))
    h2 = relus("a", (0, 2), ph, 4, T.hh2, (8, 0, 80))
    vB = b_clamp(2, av)
    h2 += relus("v", (1, 3), ph, 4, T.hh2, (8, 0, 80))
    W("a", vB)
    for t in range(3):
        ab = A(act.activation(T.Bh[:, 5 * t:5 * t + 5], BO(t, 0, 5), Act.Copy, scale=0.5))
    W("v", vB, vk)
    U2, V2, U = T.terms[:, 0:31], T.terms[:, 31:62], T.terms[:, 62:93]
    V(vec.tensor_scalar(U2, T.J2[:], BO(2, r, r + 1), None, Op.add))
    V(vec.tensor_scalar(V2, T.J2m[:], BO(2, r, r + 1), None, Op.add))
    vu = V(vec.tensor_scalar(U, T.J2[:], BO(2, r, r + 1), 0.5, Op.add, Op.mult))
    W("v", vhz, *h2)
    vch = V(vec.quantize_mx(T.C3[:, 416:544], T.C3s[:, 416:544], T.hh2[:]))
    W("v", vu)
    V(vec.tensor_scalar(T.terms[:, 93:124], U2, BO(1, r, r + 1), T.kk[:, 0:1], Op.is_lt, Op.mult))
    V(vec.tensor_scalar(T.terms[:, 124:155], V2, BO(1, r + 1, r + 2), T.kk[:, 1:2], Op.is_ge, Op.mult))
    vu = V(vec.tensor_scalar(T.terms[:, 155:186], V2, BO(2, r + 1, r + 2), 2000.0, Op.is_ge, Op.mult))
    W("v", vu)
    vu = V(vec.tensor_tensor(T.sum3[:, 0:62], T.terms[:, 62:124], T.terms[:, 124:186], Op.add))
    W("v", vu)
    vu = V(vec.tensor_tensor(T.sum1[:, 0:31], T.sum3[:, 0:31], T.sum3[:, 31:62], Op.add))
    W("v", vu)
    vl = V(vec.tensor_scalar(T.lf[:, 0:31], T.sum1[:, 0:31], 80.0, 500.0, Op.add, Op.min))
    W("v", ab)
    vN = V(vec.tensor_tensor(T.Ball[:, 0:15], T.Bh[:, 0:15], T.B0[:], Op.add))
    W("p", vc3, *ro)
    py = P(ten.matmul_mx(bank(0, 0, 416), T.qa[:], T.qas[:], T.C3[:, 0:416], T.C3s[:, 0:416], True, True))
    W("p", vch)
    pz = P(ten.matmul_mx(bank(1, 0, 128), T.qa[:], T.qas[:], T.C3[:, 416:544], T.C3s[:, 416:544], True, True))
    W("a", py)
    A(act.activation(T.YC[:, 0:416], bank(0, 0, 416), Act.Copy))
    W("a", pz)
    yc = A(act.activation(T.YC[:, 416:544], bank(1, 0, 128), Act.Copy))

    W("v", vl, vch, vc3)
    W("a", vl, vch, vc3)
    halves = ((0, 256), (256, 496))
    vf, af = [], []
    for a, b in halves:
        l = T.lf[:, a // 16:b // 16]
        vf.append(V(vec.tensor_copy(T.F[:, a:b].bitcast(dt.uint32), T.C3[:, 0:544].bitcast(dt.uint32).indirect(l))))
        af.append(A(act.activation(T.Fs[:, a:b], T.C3s[:, 0:544].indirect(l), Act.Copy)))
    W("v", yc)
    W("a", yc)
    vy = V(vec.tensor_copy(T.yt[:, 0:256], T.YC[:, 0:544].indirect(T.lf[:, 0:16])))
    ay = A(act.activation(T.yt[:, 256:496], T.YC[:, 0:544].indirect(T.lf[:, 16:31]), Act.Copy))
    W("s", vN)
    inc("dout", g.sync.dma_start(T.bd[:], T.Ball[0:1, 0:15]), 16)
    for k, (a, b) in enumerate(halves):
        W("s", vf[k])
        inc("dout", g.sync.dma_start(T.oc[:, 4 * a:4 * b], T.F[:, a:b].bitcast(dt.uint8)), 16)
    W("s", af[1])
    for i in range(4):
        inc("dout", g.sync.dma_start(T.osc[4 * i:4 * i + 4, :], T.Fs[32 * i:32 * i + 4, :]), 16)
    W("s", vy)
    inc("dout", g.sync.dma_start(T.y[:, 0:256], T.yt[:, 0:256]), 16)
    W("a", ay)
    inc("dout", act.dma_start(T.y[:, 256:496], T.yt[:, 256:496]), 16)
    W("g", *[(s, c) for s, c in cnt.items()])
